import numpy as np, ml_dtypes
CORES = [36,164,52,180,100,228,116,244]
N = 8
BF = ml_dtypes.bfloat16
W, R, Q, RO, HOP, E = 2048, 256, 12, 4, 3, 256
def parts(rng):
    v = rng.integers(0, 256, (N, 8, 16, W)); v[..., 1::8] = v[..., 0::8]
    s = 0.15 + 0.85 * rng.random((N, 8, 16, 1)); w = rng.choice(np.array([0.0, 0.1, 0.2]), (N, 8, 1, 1))
    k = np.minimum((W * s * ((1 - w) * rng.random((N, 8, 16, W)) + w * rng.random((N, 8, 1, W))) ** 2).astype(np.int64), W - 1)
    pop = np.argsort(rng.random((8, E)), axis=1)[:, :24] * 8; pop = np.concatenate([pop, pop + 1], axis=1)
    hit = np.take_along_axis(np.broadcast_to(pop, (N, 8, 48)), rng.integers(0, 48, (N, 8, 16 * R)), 2).reshape(N, 8, 16, R)
    p = np.where(rng.random((N, 8, 16, R)) < 0.3, hit, rng.integers(0, W, (N, 8, 16, R)))
    return v, k, p
def look(rng, v, p):
    o = np.take_along_axis(p, rng.integers(0, 16, (N, 8, 1, R)), 2); y = np.take_along_axis(v, o, 3)
    near = np.clip(y + rng.integers(-3, 4, y.shape) * (rng.random(y.shape) < 0.5), 0, 255)
    return np.where(rng.random((N, 8, 1, R)) < 0.75, near, rng.integers(0, 256, y.shape))
def pack(v, k, p, y):
    return {"val": np.ascontiguousarray(v.reshape(N, 128, W)).astype(np.float32).astype(BF), "clk": np.ascontiguousarray(k.reshape(N, 128, W)).astype(np.int32),
            "nam": np.ascontiguousarray(p.reshape(N, 128, R)).astype(np.int32), "seen": np.ascontiguousarray(y.reshape(N, 128, R)).astype(np.float32).astype(BF)}
def setup_inputs(rng):
    v, k, p = parts(rng)
    return pack(v, k, p, look(rng, v, p))
def setup_inputs_count(rng):
    v, k, p = parts(rng); A = W // 4; q = rng.permutation(N)
    v[q[:2]] = rng.integers(0, 256, (2, 8, 16, W)); z = rng.random((N, 8, W))
    for g in (1, 3, 5, 7):
        s = int(rng.integers(0, W - R + 1)); z[q[0], g, s:s + R] -= 1
    b = rng.integers(W // 4, W // 2, (N, 8, 16, 1)); m = np.argsort(z, axis=2); pos = np.argsort(m, axis=2)[:, :, None, :]
    n = np.where(pos < A, 16, np.where(pos < 3 * A, Q - 1, Q)); at = np.argsort(rng.random((N, 8, 16, W)), axis=2) < n
    up = (pos >= A) * rng.choice(np.array([0, 0, 1, 5]), (N, 8, 16, W))
    k = np.where(at, b + up, b - rng.integers(1, W // 8, (N, 8, 16, W)))
    def pick(lo, hi, c): return np.take_along_axis(m, rng.integers(lo, hi, (N, 8, c * R)), 2).reshape(N, 8, c, R)
    o = pick(0, A, 1); o[q[0]] = m[q[0], :, None, :R]; i = np.arange(16)[None, None, :, None]
    k0 = rng.integers(0, 16, (N, 8, 1, R)); k1 = (k0 + rng.integers(1, 16, (N, 8, 1, R))) & 15; k2 = (k0 + rng.integers(1, 16, (N, 8, 1, R))) & 15
    h = rng.integers(0, 3, (N, 8, 1, R)); h[q[0]] = 0; h[q[1]] = rng.integers(1, 3, (8, 1, R))
    p = np.where(i == k0, o, np.where(((i == k1) & (h > 0)) | ((i == k2) & (h > 1)), pick(3 * A, W, 16), pick(A, 3 * A, 16)))
    return pack(v, k, p, np.take_along_axis(v, o, 3))
def setup_inputs_crowd(rng):
    v, k, p = parts(rng); c = np.argsort(rng.random((N, 8, W)), axis=2)[..., :3]; top = np.max(k, axis=3)
    np.put_along_axis(k, np.ascontiguousarray(np.broadcast_to(c[:, :, None, :], (N, 8, 16, 3))), np.stack([top - (top >> 3), top - (top >> 4), top], axis=3), 3)
    r = np.arange(R)[None, None, None, :]; g = np.arange(8)[None, :, None, None]; i = np.arange(16)[None, None, :, None]
    star = np.where((g % 2 == 0) & (r % 2 == 1), c[:, :, None, 1:2], c[:, :, None, 0:1])
    k0 = rng.integers(0, 16, (N, 8, 1, R)); no = (r < 2) | (rng.random((N, 8, 1, R)) < 0.125)
    p = np.where(i == k0, star, np.where((i == ((k0 + 5) & 15)) & no, c[:, :, None, 2:3], p))
    return pack(v, k, p, np.take_along_axis(v, star, 3))
def setup_inputs_ends(rng):
    v, k, p = parts(rng); y = look(rng, v, p)
    p[:, 0] = p[:, 0, :1]
    p[:, 1] = rng.choice(np.array([0, 1, W - 2, W - 1]), (N, 16, R))
    k[:, 2] = (W - 1) * rng.integers(0, 2, (N, 16, W))
    v[:, 3] = 255 * (rng.random((N, 16, W)) < 0.1); y[:, 3] = 255 * (rng.random((N, 16, R)) < 0.9)
    v[:, 3, :, W // 2:] = 0; y[:, 3, :, ::2] = 255
    p[:, 4] = rng.integers(1, W - 1, (N, 16, R)); p[:, 4, 0] = 0; p[:, 4, 15] = W - 1; k[:, 4, :, 0] = 0; k[:, 4, :, W - 1] = 1; y[:, 4] = v[:, 4, :, W - 1:]
    p[:, 5, 0] = 0; k[:, 5, :, 0] = W - 1; y[:, 5] = v[:, 5, :, :1]
    v[:, 6] = 1 * (rng.random((N, 16, W)) < 0.1); y[:, 6] = 255
    h = W - R
    own = np.argsort(rng.random((N, R)), axis=1); rest = np.argsort(rng.random((N, max(h, 15 * R))), axis=1)[:, :15 * R] % h
    p7 = np.concatenate([h + own[:, None, :], rest.reshape(N, 15, R)], axis=1)
    p[:, 7] = np.take_along_axis(p7, np.argsort(rng.random((N, 16, R)), axis=1), 1)
    lead = np.argsort(rng.random((N, 16)), axis=1)[:, :, None] <= 16 - Q
    k[:, 7] = (np.where(lead, h // 2, h) * rng.random((N, 16, W)) ** 4).astype(np.int64)
    k[:, 7, :, h:] = np.where(lead, rng.integers(h // 2, h, (N, 16, R)), rng.integers(0, 9, (N, 16, R)))
    sv = rng.integers(0, 256, (16, R)); v[:, 7, :, h:] = sv; y[:, 7] = sv[:, own].transpose(1, 0, 2)
    return pack(v, k, p, y)
def setup_inputs_ties(rng):
    v, k, p = parts(rng); g = np.arange(8)[None, :, None, None]
    v = rng.integers(0, 2, (N, 8, 16, W)) + 2 * rng.integers(0, 2, (N, 8, 16, W)) * (g % 2); y = rng.integers(0, 4, (N, 8, 16, R))
    k[:, :4] = rng.integers(0, 12, (N, 4, 16, W)); p[:, 3:5] = rng.integers(0, 24, (N, 2, 16, R)) * (W // 32) + 5
    return pack(v, k, p, y)
def setup_inputs_spread(rng):
    lw = np.log2(float(W)); g = np.arange(8)[None, :, None, None]
    c = np.exp2(8 * rng.random((N, 8, 1, W))) * (rng.random((N, 8, 1, W)) > 0.0625)
    v = np.minimum((c * rng.random((N, 8, 16, W))).astype(np.int64), 255)
    z = np.where(g < 4, rng.random((N, 8, 1, W)), rng.random((N, 8, 16, 1)))
    k = np.minimum((np.exp2(lw * z) * rng.random((N, 8, 16, W))).astype(np.int64), W - 1)
    p = np.minimum(np.exp2(lw * rng.random((N, 8, 16, R))).astype(np.int64), W - 1)
    return pack(v, k, p, look(rng, v, p))
def check_inputs(d):
    bad = []
    for k in ("clk", "nam"):
        if np.min(d[k]) < 0 or np.max(d[k]) > W - 1: bad.append("range of " + k)
    for k in ("val", "seen"):
        a = d[k].astype(np.float32)
        if not np.all((a == np.floor(a)) & (a >= 0) & (a <= 255)): bad.append("whole numbers of " + k)
    return bad
def reference(val, clk, nam, seen):
    v = val.astype(np.float32).astype(np.int32).reshape(N, 8, 16, W); y = seen.astype(np.float32).astype(np.int32).reshape(N, 8, 16, R)
    kn = np.array(clk, dtype=np.int32).reshape(N, 8, 16, W); p = np.array(nam, dtype=np.int32).reshape(N, 8, 16, R)
    row = np.arange(16)[None, :, None]
    for t in range(RO):
        for a in range(N):
            b = (a + HOP * t) % N
            pa = p[a]; ix = pa.reshape(8, 1, 16 * R)
            vg = np.take_along_axis(v[b], ix, 2).reshape(8, 16, 16, R)
            kg = np.take_along_axis(kn[b], ix, 2).reshape(8, 16, 16, R)
            d = np.add.reduce(np.abs(vg - y[a][:, :, None, :]), axis=1)
            ks = np.argmin(d, axis=1)
            o = np.take_along_axis(pa, ks[:, None, :], 1)
            ko = np.take_along_axis(kg, ks[:, None, None, :], 2)
            over = (np.add.reduce((kg >= ko).astype(np.int32), axis=1) >= Q) & (pa != o)
            free = ~np.any(over, axis=1); k1 = np.argmax(over, axis=1)
            j = np.maximum.reduce(kg, axis=2)
            p1 = np.take_along_axis(pa, k1[:, None, :], 1); kf = np.take_along_axis(kg, k1[:, None, None, :], 2)[:, :, 0, :]
            back = np.where(row == ks[:, None, :], kf, np.where(row == ((ks + 1) & 15)[:, None, :], p1, pa))
            p[a] = np.where(free[:, None, :], np.maximum(pa, j), back)
            for g in range(8):
                rr = np.flatnonzero(free[g]); names, first = np.unique(o[g, 0, rr], return_index=True)
                kn[b, g][:, names] = j[g][:, rr[first]]
    return {"yp": p.reshape(N, 128, R).astype(np.float32), "yk": np.add.reduce(kn.reshape(N, 128, 8, E), axis=2).astype(np.float32)}

@@ -1,0 +1,484 @@
+from concourse.mybir import AluOpType, ActivationFunctionType
+
+W, R, RO, HOP, NR = 2048, 256, 4, 3, 8
+
+CFG = {
+    "ch": [128, 128], "bl": 2,
+    "pick": "000000001111111110010101100004021010101011011010000101010000000000000000100000002e6eb3ec101111010000000000000000aaa2a88900000000",
+    "seq": "03050n0K0p040a090I010o0b0c0G080L0f0l070x000D0m020d0e0i0u0M0v0t0z0y0s0P060N0A0O0k0w0F0J0Q0R0j0S101214210X0Y11231513161718201b0U1c19261a1u1x271d0q1e1f0h1g1t2t1h241i0V1v1Z1j1l1n1k0Z0g1E1q1w251C1D1B1y1z221o0E1p0C2s2a2b280H291G1F1H1m1I0B2c1J1K1s2d2e1L1N2f2g1O2v1M1A1Q2h2i1P2k0r1r2w1R2p1V2m1W0T1S1T1U2j2n2C2o2u2D2B2A392r2F0W2E1X2G3b37383e2H3f3c3a1Y2Y3d2I2q2J2l2M2Z2x302K2L2U2N2y3i3j3g3h2V3k2P2z312O2W2X322Q3l332R3m343n353E3B3C2S3D2T473o3p3q3s3x3r3L3u3v3I3A3w3J49483K4d4b3G4a4c3N3M3O4f3t4e3P3z4h3Q3R3F3S363H4g4i4j3V463X3U3W4k4l3Y4m4n4B3Z4D3y4A4C40414o4p4r3T4w4t4u4I4q4K4v4s5h4z42434J4H4M4F445f4L4N5g5i4O4P4Q4x5j5k4y454E5l555m4R4T4S5n5o56515e5p4G5q525r4U57584W4V5354594X4Y5s5a5t5b5u4Z505v5c5L5J5w5K5I5E5x5z5B5C5y5D6e6H5S5Q5d5R6f5P6h5U6i6k5T5V5H6g5N6j6m5W5X5Y5G6l6n5A6o6p6d5M5Z616q5F63625O6r6I6s6t6u6064656v6w696y6x6667686K6D6A6P6R6J6B6C6E6G6a6F6Q6O7l6T7m7n6b6S6U7s6V6M7q7o6c6W6z6X706Y7c7p7r7u7t6Z7w7d786L7172736N7e7v797a7f7b7x7y747z7g7A757O7B76777h7C7D7I7J7i7j7P7R7E7G7H7Q7X7F7L7W7S7K8l808n7Y8s7Z7U8m8q817N8O8o8r8p828u8t8v838w84857T868x877M898y8h8Q8S8z8P8A8B8R8C8D7k8E8L8b8I8G8X8Z8M8F8J8K8H8Y8W8T8i8j8k9l919m908892938a94958N968U97999h8c989a7V8V9b9i8d8e8f9c9d9n9o9j9k9e9p9q9r9s9u8g9v9t9f9w9x9g",
+}
+GP = ["".join("AD"[i >> b & 1] for b in range(4)) for i in range(16)]
+OPT = {"vg": GP, "kg": GP, "re": GP, "cm": ["DDDD"] + [p.lower() for p in GP[:15]], "sj": ["D+D+", "DDDD"],
+       "ks": "AD", "om": "AD", "sg": "AD", "fi": "AD", "nw": "AD", "ko": "DA", "kq": "AD", "eq": "DA", "na": "DA",
+       "vm": [0, 1], "so": [0, 1]}
+KINDS = sorted(OPT)
+H, BF, F = "float16", "bfloat16", "float32"
+
+
+def sb(n, t):
+    return ("sbuf", [128, n], t)
+
+
+SCRATCH = {"vt": sb(W, BF), "ki": sb(W, "int32"), "kt": sb(2 * (W + 32), F), "ni": sb(R, "int32"), "ys": sb(RO * R, BF),
+           "yt": sb(RO * R, BF), "yr": sb(RO * R * 16, BF), "pu": sb(RO * R, "uint16"), "po": sb(RO * R, "uint16"),
+           "pl": sb(R, F), "ph": sb(R, F), "fa": sb(512, F), "fb": sb(256, F), "fc": sb(256, F), "col": sb(144, F),
+           "j16": sb(512, BF), "e32": sb(512, BF), "pj": sb(16, "int32"), "pa": sb(16, "int32"), "pb": sb(4, "int32"),
+           "ka": sb(16, F), "cc": sb(16, F), "cs": sb(16, F), "idf": sb(128, F), "be": sb(8, BF), "bf": sb(8, BF),
+           "bg": sb(8, BF), "zs": sb(144, BF), "zb": sb(144, BF), "sm": sb(1024, BF), "nn": sb(8, F), "otc": sb(16, BF),
+           "bcm": sb(12, "uint16")}
+for _n in ("colk", "colg", "idb", "nid", "hid", "nst", "blk", "tri", "gt", "gb", "lz", "rot", "nri", "bigm", "one", "ez"):
+    SCRATCH[_n] = sb(128, BF)
+PER = {"vg": (16, BF), "ab": (16, BF), "kg": (16, H), "js": (16, H), "cm": (16, BF), "pf": (1, H), "ks": (1, BF),
+       "xo": (1, H), "ou": (1, "uint16"), "eq": (1, BF), "om": (2, F), "sg": (1, BF), "xb": (2, H), "kf": (1, H),
+       "tp": (1, H), "nw": (2, F), "ea": (2, BF), "ne": (1, BF), "rj": (1, H), "ko": (1, H)}
+SLOT = {"pm": (128, F), "st": (144, BF), "mn": (8, F), "od": (8, F), "ot": (16, "uint16"), "ta": (8, F),
+        "of": (16, "uint16"), "oo": (8, "uint16"), "kq": (128, H)}
+for _n in PER:
+    SCRATCH[_n] = sb(R * PER[_n][0], PER[_n][1])
+for _n in SLOT:
+    SCRATCH[_n] = sb(2 * SLOT[_n][0], SLOT[_n][1])
+for _b in range(8):
+    SCRATCH["ps%d" % _b] = ("psum", [128, 512], F)
+TILE = {"key": (0, 0), "kop": (0, 0), "ksp": (0, 128), "orep": (0, 256), "oot": (0, 384), "dup": (0, 392),
+        "om2": (1, 0), "cnt": (1, 192), "zz": (1, 320), "pps": (2, 0), "p1p": (2, 128), "bak": (2, 256), "otp": (2, 384)}
+
+SEMAPHORES = (["sD", "sA", "sP", "sG", "sent", "stk", "st0", "st1"] + ["ld%d" % i for i in range(4)]
+              + ["ck%d" % t for t in range(RO)] + ["a%s%d" % (x, t) for x in "yz" for t in range(1, RO)]
+              + ["ap%d%d" % (t, c) for t in range(RO) for c in range(2)])
+
+
+def A(name, c0=0, c1=None, step=1, p0=0, p1=128):
+    if c1 is None:
+        c1 = SCRATCH[name][1][1]
+    return ("ap", name, p0, p1, c0, c1, step)
+
+
+def IND(win, off):
+    return ("ind", win, off)
+
+
+def ncol(a):
+    if a[0] == "ind":
+        return 16 * ncol(a[2])
+    return len(range(a[4], a[5], a[6]))
+
+
+def isap(a):
+    return isinstance(a, tuple) and len(a) > 0 and a[0] in ("ap", "ind")
+
+
+def program(cfg):
+    ops = []
+    ch = cfg["ch"]
+    nc = len(ch)
+    base = [sum(ch[:c]) for c in range(nc)]
+    down = list(range(nc - 1, -1, -1))
+    at = [-1, 0]
+
+    def op(q, ins, name):
+        ops.append({"q": q, "ins": ins if isinstance(ins, list) else [ins], "name": name + str(at[1]), "t": at[0]})
+
+    def pick(kind):
+        return OPT[kind][int(cfg["pick"][(KINDS.index(kind) * RO + at[0]) * nc + at[1]], 16)]
+
+    def pieces(kind):
+        out = []
+        for i, q in enumerate(pick(kind)):
+            if q == "+":
+                out[-1] = (out[-1][0], out[-1][1], 512 * i + 512)
+            else:
+                out.append((q, 512 * i, 512 * i + 512))
+        return out
+
+    def nm(o): return o[1] if o[0] == "ap" else "scat"
+    def tt(o, a, b, f, x=""): op("D", ("tt", o, a, b, f), nm(o) + x)
+    def ts(o, a, s1, s2, f0, f1=None): op("D", ("ts", o, a, s1, s2, f0, f1), nm(o))
+    def act(o, a, f, b=0.0, s=1.0): op("A", ("act", o, a, f, b, s), nm(o))
+    def cp(o, a, q="D"):
+        if q == "D":
+            op("D", ("cp", o, a), nm(o))
+        else:
+            act(o, a, "Copy")
+    def ms(o, v): op("D", ("ms", o, v), nm(o))
+    def mm(terms, name):
+        op("P", [("mm", o, l, r, i == 0, i == len(terms) - 1) for i, (o, l, r) in enumerate(terms)], name)
+    def iota(o, pat, b, cm): op("G", ("iota", o, pat, b, cm), nm(o))
+
+    op("A", ("dma", A("vt"), A("val", 0, W), "ld0"), "ldv")
+    op("S", ("dma", A("ni"), A("nam", 0, R), "ld1"), "ldn")
+    op("S", ("dma", A("ys", 0, R), A("seen", 0, R), "ld2"), "lds")
+    op("S", ("dma", A("ki"), A("clk", 0, W), "ld3"), "ldk")
+    iota(A("pj"), [[1, 16]], 0, 1)
+    iota(A("col"), [[1, 144]], 0, 0)
+    iota(A("j16"), [[1, 32], [0, 16]], 0, 0)
+    iota(A("colk"), [[0, 8], [1, 16]], 0, 0)
+    iota(A("colg"), [[16, 8], [0, 16]], 0, 0)
+    ts(A("pa"), A("pj"), 15, None, "bitwise_and")
+    ts(A("pb", 0, 1), A("pj", 0, 1), 31, None, "bitwise_and")
+    cp(A("ka"), A("pa"))
+    acol = A("ka", 0, 1)
+    tt(A("cs", 0, 1), A("pj", 0, 1), A("pa", 0, 1), "subtract")
+    g16 = A("cs", 0, 1)
+    cp(A("cs", 1, 2), A("pb", 0, 1))
+    ts(A("cc"), A("ka"), g16, None, "add")
+    ts(A("cs", 2, 3), g16, 15.0, None, "add")
+    ts(A("cs", 3, 4), acol, -0.5, 0.5, "mult", "add")
+    ts(A("cs", 6, 7), acol, float(W), None, "add")
+    c128, me = A("col", 0, 128), A("cc", 0, 1)
+    ts(A("idb"), c128, me, None, "is_equal")
+    act(A("nid"), A("idb"), "Copy", 0.0, -1.0)
+    ts(A("e32"), A("j16"), A("cs", 1, 2), None, "is_equal")
+    ts(A("be"), A("colg", 0, 128, 16), g16, 16.0, "is_equal", "mult")
+    act(A("one"), A("colk"), "Copy", 1.0, 0.0)
+    ms(A("bigm"), 0.0)
+    ms(A("bigm", 0, 128, 16), 1048576.0)
+    cp(A("bcm", 0, 8), A("col", 0, 8))
+    cp(A("bcm", 8, 12), A("col", 0, 8, 2))
+    ts(A("cs", 7, 8), acol, W + 16.0, None, "add")
+    act(A("ez"), A("colk"), "Relu", 1.0, -1.0)
+    ts(A("blk"), A("colg"), g16, None, "is_equal")
+    act(A("idf"), A("idb"), "Copy")
+    act(A("nst"), A("idb"), "Copy", 0.0, -16.0)
+    ts(A("tri"), A("colk"), acol, 8192.0, "is_le", "mult")
+    ts(A("gt"), A("colk"), acol, 0.5, "is_gt", "mult")
+    act(A("hid"), A("idb"), "Copy", 0.0, 0.5)
+    tt(A("gb"), A("gt"), A("blk"), "mult")
+    tt(A("lz"), A("hid"), A("gb"), "subtract")
+    ts(A("rot"), c128, A("cc", 1, 2), None, "is_equal")
+    ts(A("nri"), c128, A("cc", 15, 16), -1.0, "is_equal", "mult")
+    ts(A("zs"), A("col"), A("cs", 2, 3), None, "is_equal")
+    act(A("zb"), A("zs"), "Copy", 0.0, 4096.0)
+    iota(A("sm"), [[0, 64], [2048, 16]], 0, 0)
+    ts(A("nn"), A("col", 0, 8), 16.0, acol, "mult", "add")
+    ts(A("otc", 0, 8), A("nn"), 8192.0, None, "mult")
+    for c in down:
+        ms(A("st", 144 * c, 144 * c + 16), 1.0)
+    ms(A("kt", W, W + 32), 0.0)
+    ms(A("kt", 2 * W + 32, 2 * W + 64), 0.0)
+    for h in (1, 0):
+        cp(A("pu", 128 * h, 128 * h + 128), A("ni", 128 * h, 128 * h + 128))
+        mm([(A("ps%d" % h, 0, 128), A("ys", 128 * h, 128 * h + 128), A("idb"))], "yT")
+        cp(A("yt", 128 * h, 128 * h + 128), A("ps%d" % h, 0, 128), "A")
+    act(A("bf"), A("be"), "Copy", 0.0, 2.0)
+    act(A("bg"), A("be"), "Copy", 0.0, -1.0)
+    for t in range(1, RO):
+        ways = set()
+        for c in down:
+            at[:] = [t, c]
+            ways.add(pick("vm"))
+        at[:] = [-1, 0]
+        if 0 in ways:
+            op("G", ("rdma", A("yt", t * R, t * R + R), A("yt", 0, R), HOP * t, "ay%d" % t), "sendy")
+        if 1 in ways:
+            op("G", ("rdma", A("ys", t * R, t * R + R), A("ys", 0, R), HOP * t, "az%d" % t), "sendy")
+    cp(A("kt", 0, 1024), A("ki", 0, 1024))
+    cp(A("kt", 1024, W), A("ki", 1024, W))
+
+    def sel(a): return A("zs", 15 - a, 143 - a)
+    def big(a): return A("zb", 15 - a, 143 - a)
+    wide = [0]
+
+    def turn():
+        wide[0] += 1
+        return A("ps%d" % (1 - wide[0] % 2))
+
+    def chunk(c):
+        def B(name, a=0, b=None, step=1, p1=128):
+            w, o = (PER[name][0] * ch[c], PER[name][0] * base[c]) if name in PER else (SLOT[name][0], SLOT[name][0] * c)
+            return A(name, o + a, o + (w if b is None else b), step, 0, p1)
+        return B
+
+    for t in range(RO):
+        at[:] = [t, 0]
+        k0, k1 = (W + 32) * (t % 2), (W + 32) * (1 - t % 2)
+        KT = A("kt", k0, k0 + W)
+        op("S", ("dma", A("kt", k1, k1 + W), KT, "ck%d" % t), "cpk")
+        for c in down:
+            at[:] = [t, c]
+            n, m, B = ch[c], ch[c] // 16, chunk(c)
+            x = n // 2 if cfg["bl"] == 2 else 0
+            def S(name, a=0, b=n, step=1, p1=128):
+                return A("ps%d" % (2 + 3 * c + TILE[name][0]), TILE[name][1] + a, TILE[name][1] + b, step, 0, p1)
+            ksp, orep, pps, om2, cnt, zz, p1p, bak = (S(k) for k in ("ksp", "orep", "pps", "om2", "cnt", "zz", "p1p", "bak"))
+            key, oot, dup = S("key", 0, 128), S("oot", 0, m), S("dup", 0, m)
+            pc = t * R + base[c]
+            def PU(a, b): return A("pu", pc + a // 16, pc + b // 16)
+            PF = B("pf")
+            cp(PF, A("pu", pc, pc + n))
+            flat = pick("vm")
+            both = flat and "D" in pick("re")
+            for k in range(16 if flat else 0):
+                op("G", ("rep", A("yr", 16 * pc + k, 16 * (pc + n), 16), A("ys", pc, pc + n)), "yr")
+            for q, a, b in pieces("re") if flat else []:
+                tt(B("vg", a, b), IND(A("vt"), PU(a, b)), A("yr", 16 * pc + a, 16 * pc + b), "subtract")
+                if q == "A":
+                    act(B("ab", a, b), B("vg", a, b), "Relu" if both else "Abs")
+                else:
+                    ts(B("ab", a, b), B("vg", a, b), 0.0, None, "max")
+            for q, a, b in [] if flat else pieces("vg"):
+                cp(B("vg", a, b), IND(A("vt"), PU(a, b)), q)
+            for q in range(0 if flat else n // 32):
+                wb = turn()
+                u = base[c] // 32 + q
+                y0, p0 = t * R + 128 * (u // 4), 32 * (u % 4)
+                mm([(wb, A("yt", y0, y0 + 128, 1, p0, p0 + 32), A("e32", 0, 512, 1, p0, p0 + 32)),
+                    (wb, A("nid"), B("vg", 512 * q, 512 * q + 512))], "diff")
+                act(B("ab", 512 * q, 512 * q + 512), wb, "Abs")
+            mm([(key, A("one", 0, 128, 1, 0, 1), A("colk", 0, 128, 1, 0, 1))]
+               + [(S("key", k, 128, 16, n), B("vg", k, 16 * n, 16), A("bg")) for k in range(16 if both else 0)]
+               + [(S("key", k, 128, 16, n), B("ab", k, 16 * n, 16), A("bf" if both else "be")) for k in range(16)], "key")
+            op("D", ("scan", B("pm"), A("bigm"), key, 0.0, "add", "min"), "pm")
+            cp(B("mn"), B("pm", 15, 128, 16))
+            tt(B("st", 16, 144), IND(B("mn"), A("bcm", 0, 8)), B("pm"), "is_equal")
+            mm([(ksp, B("st", 16, 144, 1, n), A("idb", 0, n, 1, 0, n)), (ksp, B("st", 15, 143, 1, n), A("nid", 0, n, 1, 0, n)),
+                (ksp, A("ez", 0, 128, 1, 0, 1), A("one", 0, n, 1, 0, 1))], "ksp")
+            tt(B("xo"), ksp, PF, "mult")
+            mm([(orep, A("blk"), B("xo"))], "orep")
+            fused = pick("cm")[0] == "D"
+            mm([(oot, sel(a), B("xo", a, n, 16)) for a in range(16)], "oot")
+            if fused:
+                op("D", ("cp", B("ou"), orep), "ou")
+            else:
+                op("D", ("cp", B("oo", 0, m), oot), "ou")
+                cp(B("ko"), IND(KT, B("oo", 0, m)), pick("ko"))
+                mm([(S("kop", 0, 128, 1, n), B("ko"), A("idb"))], "kop")
+                cp(B("kq", 0, 128, 1, n), S("kop", 0, 128, 1, n), pick("kq"))
+            cp(B("ks"), ksp, pick("ks"))
+            if pick("eq") == "D":
+                tt(B("eq"), orep, PF, "is_equal")
+            else:
+                mm([(zz, A("nid"), PF), (zz, A("blk"), B("xo"))], "eqp")
+                act(B("ne"), zz, "Abs")
+                act(B("eq"), B("ne"), "Relu", 1.0, -1.0)
+            mm([(om2, A("idb"), A("tri", 0, n)), (om2, A("blk"), B("xo"))]
+               + [(S("om2", n + 16 * j, n + 16 * j + 16), A("blk"), B("xo", 32 * j + 16, 32 * j + 32)) for j in range(x // 16)], "omp")
+            cp(B("om", 0, n + x), S("om2", 0, n + x), pick("om"))
+            tt(B("od", 0, m), oot, A("otc", 0, m), "subtract")
+            mm([(pps, A("idb"), PF)], "pps")
+            for q, a, b in pieces("kg"):
+                cp(B("kg", a, b), IND(KT, PU(a, b)), q)
+            for q, a, b in pieces("sj"):
+                op("D", ("scan", B("js", a, b), A("sm", 0, b - a), B("kg", a, b), 0.0, "min", "max"), "js")
+            if pick("na") == "D":
+                tt(B("nw", 0, 2 * n, 2), pps, B("js", 15, 16 * n, 16), "max", "a")
+            else:
+                mm([(bak, A("nid"), PF), (bak, A("idb"), B("js", 15, 16 * n, 16))], "nwa")
+                act(B("rj"), bak, "Relu")
+                mm([(bak, A("idb"), PF), (bak, A("idb"), B("rj"))], "nwa")
+                op("A", ("act", B("nw", 0, 2 * n, 2), bak, "Copy", 0.0, 1.0), "nwa")
+            for q, a, b in pieces("cm"):
+                if fused:
+                    tt(B("cm", a, b), IND(KT, B("ou", a // 16, b // 16)), B("kg", a, b), "is_le")
+                    continue
+                wb = turn()
+                p0 = a // 16
+                mm([(wb, ("ap", "kq", p0, p0 + 32, 128 * c, 128 * c + 128, 1), A("e32", 0, 512, 1, p0, p0 + 32)),
+                    (wb, A("nid"), B("kg", a, b))], "dik")
+                if q == "a":
+                    act(B("cm", a, b), wb, "Sign", 0.5, -1.0)
+                else:
+                    ts(B("cm", a, b), wb, 0.0, 2.0, "is_le", "mult")
+            for a in range(0, n, 64):
+                b = min(n, a + 64)
+                o = S("cnt", a, b)
+                fix = [(S("cnt", u, u + 32), A("nst"), A("one", 0, 32)) for u in range(a, b, 32) if pick("cm")[u // 32] == "d"]
+                mm([(o, A("nst"), B("eq", a, b))] + fix
+                   + [(o, sel(k), B("cm", 16 * a + k, 16 * b, 16)) for k in range(16)], "cnt")
+            if pick("sg") == "A":
+                act(B("sg"), cnt, "Sign", -11.5 if fused else -7.0, 1.0)
+                hb = A("cs", 3, 4)
+            else:
+                ts(B("sg"), cnt, 11.5 if fused else 7.0, 2.0, "is_ge", "mult")
+                hb = 0.0
+            mm([(zz, A("lz"), B("sg"))], "zz")
+            if pick("fi") == "A":
+                act(B("xb", 0, n), zz, "Relu", hb, 1.0)
+            else:
+                ts(B("xb", 0, n), zz, hb, 0.0, "add", "max")
+            o1, o2, otp = S("otp", 0, m), S("otp", m, 2 * m), S("otp", 0, 2 * m)
+            first = (o1, A("idb"), A("otc", 0, m))
+            if pick("so"):
+                mm([first] + [(o1, big(a), B("xb", a, n, 16)) for a in range(16)], "otp")
+                tt(B("ta", 0, m), o1, B("od", 0, m), "add")
+            tt(B("xb", n, 2 * n), pps, B("xb", 0, n), "mult", "p")
+            if pick("so"):
+                mm([(o2, big(a), B("xb", n + a, 2 * n, 16)) for a in range(16)], "otp")
+            else:
+                mm([first, (o2, A("idb"), A("bigm", 1, 1 + m))]
+                   + [(otp, big(a), B("xb", a, 2 * n, 16)) for a in range(16)], "otp")
+                tt(B("ta", 0, m), o1, B("od", 0, m), "add")
+            mm([(p1p, A("nri"), PF), (p1p, A("blk"), B("xb", n, 2 * n))], "ppp")
+            ts(B("ot", 0, 2 * m), otp, 1.0 / 4096, None, "mult")
+            tt(B("tp"), p1p, B("ks"), "mult")
+            tt(B("kf"), IND(KT, B("ot", m, 2 * m)), B("ks"), "mult")
+            mm([(bak, A("idb"), PF), (bak, A("nid"), B("xo")), (bak, A("rot"), B("tp")), (bak, A("idb"), B("kf"))], "bak")
+            cp(B("nw", 1, 2 * n, 2), bak, pick("nw"))
+            if t < RO - 1:
+                src, dst, hop = A("po", pc, pc + n), A("pu", pc + R, pc + R + n), HOP
+            else:
+                src, dst, hop = A("pl", base[c], base[c] + n), A("ph", base[c], base[c] + n), -HOP * t
+            op("D", ("cp", src, IND(B("nw"), B("ot", 0, m))), "po")
+            op("G", ("rdma", dst, src, hop, "ap%d%d" % (t, c)), "sendp")
+            if t == RO - 1:
+                op("S", ("dma", A("yp", base[c], base[c] + n), dst, "st%d" % c), "stp")
+            tt(B("ea", 0, n + x), IND(B("ta", 0, m), A("bcm", 0, m + x // 16)), B("om", 0, n + x), "is_equal")
+            mm([(dup, A("idf"), B("ta", 0, m))] + [(dup, big(a), B("ea", a, n, 16)) for a in range(16)]
+               + [(S("dup", 1, m, 2), big(a), B("ea", n + a, n + x, 16)) for a in range(16 if x else 0)], "dup")
+            if x:
+                for j in range(2):
+                    ts(B("of", j, m, 2), S("dup", j, m, 2), A("cs", 6 + j, 7 + j), None, "min")
+            else:
+                ts(B("of", 0, 2 * m, 2), dup, A("cs", 6, 7), None, "min")
+        for c in down:
+            at[:] = [t, c]
+            B = chunk(c)
+            u = cfg["bl"]
+            for m in range(ch[c] // (16 * u) - 1, -1, -1):
+                cp(IND(A("kt", k1, k1 + W + 32), B("of", 2 * m, 2 * m + u)), B("js", 256 * u * m + 15, 256 * u * (m + 1), 16))
+    fo = A("ps0", 0, 256)
+    mm([(fo, A("idf"), A("kt", 256 * b, 256 * b + 256)) for b in range(4)], "fold")
+    tt(A("fa"), A("kt", 1024, 1536), A("kt", 1536, 2048), "add")
+    tt(A("fb"), A("fa", 0, 256), A("fa", 256, 512), "add")
+    tt(A("fc"), fo, A("fb"), "add")
+    op("S", ("dma", A("yk", 0, 256), A("fc"), "stk"), "stk")
+    return ops
+
+
+def links(ops):
+    hist = {}
+    for x, o in enumerate(ops):
+        wr, rd = set(), set()
+        for i in o["ins"]:
+            for n, a in enumerate(y for y in i[1:] if isap(y)):
+                if a[0] == "ind":
+                    rd.add((a[2][1], a[2][4], a[2][5]))
+                    a = a[1]
+                (rd if n else wr).add((a[1], a[4], a[5]))
+        o["banks"] = sorted(set(r[0] for r in wr | rd if r[0].startswith("ps")))
+        o["dma"] = o["ins"][0][0] in ("dma", "rdma")
+        dep = {}
+        for regs, mine in ((rd, False), (wr, True)):
+            for nm, lo, hi in regs:
+                for y, l2, h2, w2 in hist.get(nm, []):
+                    if l2 < hi and lo < h2 and (mine or w2) and not (nm == "yr" and mine):
+                        dep[y] = dep.get(y, False) or (w2 and not mine)
+        o["dep"] = dep
+        for regs, mine in ((rd, False), (wr, True)):
+            for nm, lo, hi in sorted(regs):
+                h = hist.setdefault(nm, [])
+                if mine and nm != "yr":
+                    h[:] = [e for e in h if not (lo <= e[1] and e[2] <= hi)]
+                h.append((x, lo, hi, mine))
+
+
+def plan(cfg):
+    ops = program(cfg)
+    links(ops)
+    al = "0123456789abcdefghijklmnopqrstuvwxyzABCDEFGHIJKLMNOPQRSTUVWXYZ"
+    s = cfg["seq"]
+    order = {q: [] for q in "DAPGS"}
+    total = {q: 0 for q in "DAPG"}
+    seen = {q: {} for q in order}
+    last = {}
+    for x in [al.index(s[i]) * 62 + al.index(s[i + 1]) for i in range(0, len(s), 2)]:
+        o = ops[x]
+        q = o["q"]
+        wait = [y for y, raw in o["dep"].items() if raw or ops[y]["q"] != q or q != "P"]
+        for b in o["banks"]:
+            wait += [y for q2, y in last.get(b, {}).items() if q2 != q]
+            last.setdefault(b, {})[q] = x
+        need = {}
+        for y in wait:
+            sem, v = ops[y]["sig"]
+            if v > seen[q].get(sem, 0):
+                need[sem] = max(v, need.get(sem, 0))
+        seen[q].update(need)
+        o["need"] = sorted(need.items())
+        if not o["dma"]:
+            total[q] += 1
+            o["sig"] = ("s" + q, total[q])
+        else:
+            o["sig"] = (o["ins"][0][3], 16) if o["ins"][0][0] == "dma" else (o["ins"][0][4], 1)
+        order[q].append(x)
+    assert sum(len(v) for v in order.values()) == len(ops)
+    return ops, order, total
+
+
+MEMO = {}
+
+
+def rank_program(g, core, T, topo):
+    rank = T.rank_of(core)
+    if rank is None:
+        return
+    if "plan" not in MEMO:
+        MEMO["plan"] = plan(CFG)
+    ops, order, total = MEMO["plan"]
+    cores = T.cores
+    queue = {"D": g.vector, "A": g.scalar, "P": g.tensor, "G": g, "S": g.sync}
+    alu = {"add": AluOpType.add, "subtract": AluOpType.subtract, "mult": AluOpType.mult, "max": AluOpType.max,
+           "min": AluOpType.min, "is_equal": AluOpType.is_equal, "is_le": AluOpType.is_le, "is_gt": AluOpType.is_gt,
+           "is_ge": AluOpType.is_ge, "bitwise_and": AluOpType.bitwise_and}
+    fn = {"Copy": ActivationFunctionType.Copy, "Abs": ActivationFunctionType.Abs, "Sign": ActivationFunctionType.Sign,
+          "Relu": ActivationFunctionType.Relu}
+
+    def ap(a):
+        if not isap(a):
+            return a
+        if a[0] == "ind":
+            return ap(a[1]).indirect(ap(a[2]))
+        if a[6] == 1:
+            return T[a[1]][a[2]:a[3], a[4]:a[5]]
+        return T[a[1]][a[2]:a[3], a[4]:a[5]:a[6]]
+
+    arrive = {o["ins"][0][4]: len(topo.engines(cores[(rank - o["ins"][0][3]) % NR], core))
+              for o in ops if o["ins"][0][0] == "rdma"}
+    sent = 0
+    for q in "SAGPD":
+        e = queue[q]
+        for x in order[q]:
+            o = ops[x]
+            for sem, v in o["need"]:
+                e.wait_ge(T.sem[sem], arrive.get(sem, v))
+            for i in o["ins"]:
+                k = i[0]
+                a = [ap(y) for y in i[1:]]
+                if k == "dma":
+                    e.dma_start(a[0], a[1]).then_inc(T.sem[i[3]], 16)
+                    continue
+                if k == "rdma":
+                    dst = cores[(rank + i[3]) % NR]
+                    rid, pid = topo.addr(dst, core)
+                    e.remote_dma(a[0], a[1], T.sem[i[4]], T.sem.sent, pid, rid, topo.mask(core, dst))
+                    sent += len(topo.engines(core, dst))
+                    continue
+                if k == "mm":
+                    h = e.matmul(a[0], a[1], a[2], a[3], a[4])
+                elif k == "tt":
+                    h = e.tensor_tensor(a[0], a[1], a[2], alu[a[3]])
+                elif k == "ts":
+                    if a[5] is None:
+                        h = e.tensor_scalar(a[0], a[1], a[2], None, alu[a[4]])
+                    else:
+                        h = e.tensor_scalar(a[0], a[1], a[2], a[3], alu[a[4]], alu[a[5]])
+                elif k == "cp":
+                    h = e.tensor_copy(a[0], a[1])
+                elif k == "scan":
+                    h = e.tensor_tensor_scan(a[0], a[1], a[2], a[3], alu[a[4]], alu[a[5]])
+                elif k == "rep":
+                    h = e.affine_select(a[0], a[1], [[0, ncol(i[1])]], AluOpType.is_gt, 0.0, 1, 0)
+                elif k == "ms":
+                    h = e.memset(a[0], a[1])
+                elif k == "act":
+                    h = e.activation(a[0], a[1], fn[a[2]], bias=a[3], scale=a[4])
+                elif SCRATCH[i[1][1]][2] == "int32":
+                    h = e.iota(a[0], a[1], a[2], a[3])
+                else:
+                    h = e.iota(a[0], a[1], a[2], a[3], allow_small_or_imprecise_dtypes=True)
+                if i is o["ins"][-1]:
+                    h.then_inc(T.sem["s" + q], 1)
+    for q in "DAPG":
+        g.wait_ge(T.sem["s" + q], total[q])
+    g.wait_ge(T.sem.sent, sent)
+    for s in ("stk", "st0", "st1"):
+        g.wait_ge(T.sem[s], 16)

@@ -1,49 +1,44 @@
 from concourse.mybir import AluOpType, ActivationFunctionType
 
 W, R, RO, HOP, NR = 2048, 256, 4, 3, 8
+PAD, SPARE = 8, 32
+TW = PAD + W + SPARE
+H, BF, F, U16, I32 = "float16", "bfloat16", "float32", "uint16", "int32"
+CH = 128
 
-CFG = {
-    "ch": [128, 128], "bl": 2,
-    "pick": "000000001111111110010101100004021010101011011010000101010000000000000000100000002e6eb3ec101111010000000000000000aaa2a88900000000",
-    "seq": "03050n0K0p040a090I010o0b0c0G080L0f0l070x000D0m020d0e0i0u0M0v0t0z0y0s0P060N0A0O0k0w0F0J0Q0R0j0S101214210X0Y11231513161718201b0U1c19261a1u1x271d0q1e1f0h1g1t2t1h241i0V1v1Z1j1l1n1k0Z0g1E1q1w251C1D1B1y1z221o0E1p0C2s2a2b280H291G1F1H1m1I0B2c1J1K1s2d2e1L1N2f2g1O2v1M1A1Q2h2i1P2k0r1r2w1R2p1V2m1W0T1S1T1U2j2n2C2o2u2D2B2A392r2F0W2E1X2G3b37383e2H3f3c3a1Y2Y3d2I2q2J2l2M2Z2x302K2L2U2N2y3i3j3g3h2V3k2P2z312O2W2X322Q3l332R3m343n353E3B3C2S3D2T473o3p3q3s3x3r3L3u3v3I3A3w3J49483K4d4b3G4a4c3N3M3O4f3t4e3P3z4h3Q3R3F3S363H4g4i4j3V463X3U3W4k4l3Y4m4n4B3Z4D3y4A4C40414o4p4r3T4w4t4u4I4q4K4v4s5h4z42434J4H4M4F445f4L4N5g5i4O4P4Q4x5j5k4y454E5l555m4R4T4S5n5o56515e5p4G5q525r4U57584W4V5354594X4Y5s5a5t5b5u4Z505v5c5L5J5w5K5I5E5x5z5B5C5y5D6e6H5S5Q5d5R6f5P6h5U6i6k5T5V5H6g5N6j6m5W5X5Y5G6l6n5A6o6p6d5M5Z616q5F63625O6r6I6s6t6u6064656v6w696y6x6667686K6D6A6P6R6J6B6C6E6G6a6F6Q6O7l6T7m7n6b6S6U7s6V6M7q7o6c6W6z6X706Y7c7p7r7u7t6Z7w7d786L7172736N7e7v797a7f7b7x7y747z7g7A757O7B76777h7C7D7I7J7i7j7P7R7E7G7H7Q7X7F7L7W7S7K8l808n7Y8s7Z7U8m8q817N8O8o8r8p828u8t8v838w84857T868x877M898y8h8Q8S8z8P8A8B8R8C8D7k8E8L8b8I8G8X8Z8M8F8J8K8H8Y8W8T8i8j8k9l919m908892938a94958N968U97999h8c989a7V8V9b9i8d8e8f9c9d9n9o9j9k9e9p9q9r9s9u8g9v9t9f9w9x9g",
-}
-GP = ["".join("AD"[i >> b & 1] for b in range(4)) for i in range(16)]
-OPT = {"vg": GP, "kg": GP, "re": GP, "cm": ["DDDD"] + [p.lower() for p in GP[:15]], "sj": ["D+D+", "DDDD"],
-       "ks": "AD", "om": "AD", "sg": "AD", "fi": "AD", "nw": "AD", "ko": "DA", "kq": "AD", "eq": "DA", "na": "DA",
-       "vm": [0, 1], "so": [0, 1]}
-KINDS = sorted(OPT)
-H, BF, F = "float16", "bfloat16", "float32"
+ST = {'per': [{'vg':'A+D+D+D+','re':'AAAAAAAA','kg':'A+A+A+D+','cm':'DDAA','sj': 2,'ko':'A','ks':'A','eq':'A','sg':'A','r':'A','jp':'D','o3':'D','ea':'D','bl': 1,'pn':'S','bs': 0,'pp': 1},{'vg':'D+D+A+A+','re':'A+A+A+A+','kg':'A+++A+++','cm':'DDAA','sj': 2,'ko':'D','ks':'A','eq':'A','sg':'D','r':'A','jp':'A','o3':'D','ea':'D','bl': 1,'pn':'S','pp': 1,'bs': 0}],'r0': [{'yr':'G','re':'AA+A+A+A','sj': 2,'ko':'D','sg':'A','ks':'A','ea':'A','r':'A','o3':'A','eq':'D','jp':'A','cm':'DDAA','kg':'A+++A+D+','vg':'A+d+d+d+','bl': 2,'pn':'S','pp': 0,'bs': 0},{'yr':'A','ko':'D','r':'D','ea':'A','eq':'D','ks':'A','kg':'A+A+A+A+','sg':'A','vg':'d+d+A+A+','jp':'D','o3':'D','sj': 2,'cm':'DDAA','bl': 1,'pn':'S','re':'A+A+A+A+','pp': 0}],'r3': [{},{}],'x': {'kc':'GD'},'T': 17400,'phi':'4lR4Sk4pH4Zz4mf50b4as56O5Ki6UE4Fm4mG3pp2uA3ZQ4y53eE3kq2XW52o5Os4Fw5Tm52661E4Il5Ws55y5YZ54J60s4Qi5N059V6212ts2B12yU3Mo2ui4yT37k5Gx4Gu4p34GV57I2AI3qS3Rj3bX3kK3Gy4tA3DJ2Su3II3l24wz3903YP3Xi4Sb2PM4UP5FP4YY5K24VK5Fi4UM5Pp6507hJ4au3WE4e651D4lJ4Dd4jP53S3Tg3bP41v49A5MK6JD3bA53b5xN33w3Gp2WQ4sg38g2Yj5Ke70S5D86b155o6985s264w2we42X58r5MO6xp4Pv57z4Ic5q94Pw57t4Id4Tp5Fh4Tn5zn5mC5zq4jf5gN2v94D62Cs4u33Kr4Cn08j08o08408908e57K5Go5V84i63em5se6HL3OF4MC3cp56N6906dk7lP2vs4Tx5xp4gF5lF4Tf5Bb5Hb6nG5Bu6bG5D46c23HZ2r32tt4td5gu2ml4Gl4Uw5XP7h23Jv3l85qF6bR4P26c36oM6n173U6sG5OB6S06Oo6K079O7hc7mJ6eQ6hw2KC40s3LN3Wx5c862m2hl3WL4W24E759A3dL5Kf6y04mF4wy4kt51t4gd50t4f84nN2Hw2Au2LJ58y69o5DA6474IR57A2J82Wb4GQ5iu68N9wqa4w8Dwa4L9es9Iua4xauRbJq9WPaqA9ZwaYi9Y1aKXa2iawva40b2Ha5Ya6x9itaEL9uYaOF8xl9TeaJ19V7b0m9Sx9tT9uaai4a70bwa9DYa3o8v2ak1b3cehXec3ej3erpejjernenveijecMe5x9YmaHYeeJawmbxwa8vbuM9ZjayRa7MaoA9oma77anYbse9Tqak89TPanAaxiaLr9E3a0T9TpaJjafuaGz94yatLaa2ax99Xoakk9BWaGxas7bEY9BraGt93Qa8h9IvaxRabOaZna6WaFbajhaz4aG5bJ38SCanyaFpbMs9E19Lw8sE9E2a5BabIatFbIIaVNbJbaxCbQNauibPtaUabNfbqBbSvbtdbAdbDxbtzb8Bby59SQbaO8ASapxaX2cpSaswbxv8DN9XJ8Qk9Zn8ZXa7x8Y59TG9Nyakia78aKo8B7av77CR8cJ6D56fB8Ct6iS6kV7ZG6zM6MY6BR7cz6CR6UI7yW7Cu9sWaJx'}
 
 
 def sb(n, t):
     return ("sbuf", [128, n], t)
 
 
-SCRATCH = {"vt": sb(W, BF), "ki": sb(W, "int32"), "kt": sb(2 * (W + 32), F), "ni": sb(R, "int32"), "ys": sb(RO * R, BF),
-           "yt": sb(RO * R, BF), "yr": sb(RO * R * 16, BF), "pu": sb(RO * R, "uint16"), "po": sb(RO * R, "uint16"),
-           "pl": sb(R, F), "ph": sb(R, F), "fa": sb(512, F), "fb": sb(256, F), "fc": sb(256, F), "col": sb(144, F),
-           "j16": sb(512, BF), "e32": sb(512, BF), "pj": sb(16, "int32"), "pa": sb(16, "int32"), "pb": sb(4, "int32"),
-           "ka": sb(16, F), "cc": sb(16, F), "cs": sb(16, F), "idf": sb(128, F), "be": sb(8, BF), "bf": sb(8, BF),
-           "bg": sb(8, BF), "zs": sb(144, BF), "zb": sb(144, BF), "sm": sb(1024, BF), "nn": sb(8, F), "otc": sb(16, BF),
-           "bcm": sb(12, "uint16")}
-for _n in ("colk", "colg", "idb", "nid", "hid", "nst", "blk", "tri", "gt", "gb", "lz", "rot", "nri", "bigm", "one", "ez"):
+SCRATCH = {"vt": sb(W, BF), "ki": sb(W, I32), "kt": sb(2 * TW, F), "ni": sb(R, I32), "ys": sb(RO * 2 * R, BF),
+           "e32": sb(512, BF), "pb": sb(4, I32), "p4": sb(4, I32),
+           "yr": sb(RO * R * 16, BF), "pf": sb(RO * R, H), "po": sb(RO * R, H), "pu": sb(R, U16),
+           "pl": sb(R, F), "ph": sb(R, F), "fa": sb(256, F), "fc": sb(256, F), "fh": sb(W, H), "col": sb(144, F),
+           "pj": sb(16, I32), "pa": sb(16, I32), "ka": sb(16, F), "cc": sb(16, F), "cs": sb(32, F),
+           "idf": sb(128, F), "be": sb(8, BF), "bf": sb(8, BF), "bg": sb(8, BF), "zs": sb(144, BF),
+           "sm": sb(1024, BF), "end": sb(8, U16), "dd": sb(2048, BF), "wg": sb(16, F), "wh": sb(16, F)}
+for _n in ("colk", "colg", "idb", "nid", "nst", "blk", "gt", "gb", "lz", "rot", "nri", "bigm", "one", "ez", "bb", "nbb",
+           "neg", "big", "bid"):
     SCRATCH[_n] = sb(128, BF)
-PER = {"vg": (16, BF), "ab": (16, BF), "kg": (16, H), "js": (16, H), "cm": (16, BF), "pf": (1, H), "ks": (1, BF),
-       "xo": (1, H), "ou": (1, "uint16"), "eq": (1, BF), "om": (2, F), "sg": (1, BF), "xb": (2, H), "kf": (1, H),
-       "tp": (1, H), "nw": (2, F), "ea": (2, BF), "ne": (1, BF), "rj": (1, H), "ko": (1, H)}
-SLOT = {"pm": (128, F), "st": (144, BF), "mn": (8, F), "od": (8, F), "ot": (16, "uint16"), "ta": (8, F),
-        "of": (16, "uint16"), "oo": (8, "uint16"), "kq": (128, H)}
+PER = {"vg": (16, BF), "ab": (16, BF), "kg": (16, H), "js": (16, H), "cm": (16, BF), "ks": (1, BF), "xo": (1, H),
+       "eq": (1, BF), "ne": (1, BF), "sg": (1, BF), "r": (1, H), "kf": (1, H), "tp": (1, H), "mx": (1, H), "jp": (1, F),
+       "ea": (2, BF), "nf": (2, BF), "ko": (1, H)}
+SLOT = {"pm": (128, F), "pn": (128, F), "st": (144, BF), "oo": (8, U16), "o3": (8, H), "ot": (8, U16), "of": (16, U16)}
 for _n in PER:
     SCRATCH[_n] = sb(R * PER[_n][0], PER[_n][1])
 for _n in SLOT:
     SCRATCH[_n] = sb(2 * SLOT[_n][0], SLOT[_n][1])
 for _b in range(8):
     SCRATCH["ps%d" % _b] = ("psum", [128, 512], F)
-TILE = {"key": (0, 0), "kop": (0, 0), "ksp": (0, 128), "orep": (0, 256), "oot": (0, 384), "dup": (0, 392),
-        "om2": (1, 0), "cnt": (1, 192), "zz": (1, 320), "pps": (2, 0), "p1p": (2, 128), "bak": (2, 256), "otp": (2, 384)}
+TILE = {"key": (0, 0), "oot": (0, 0), "dup": (0, 8), "ksp": (0, 128), "x": (0, 256), "pps": (1, 256),
+        "cnt": (1, 0), "jpp": (1, 0), "zz": (1, 128), "otp": (1, 128), "p1p": (1, 256), "orep": (1, 384), "bak": (1, 384)}
+NWIDE = 4
 
-SEMAPHORES = (["sD", "sA", "sP", "sG", "sent", "stk", "st0", "st1"] + ["ld%d" % i for i in range(4)]
-              + ["ck%d" % t for t in range(RO)] + ["a%s%d" % (x, t) for x in "yz" for t in range(1, RO)]
+SEMAPHORES = (["sD", "sA", "sP", "sG", "sent", "stk", "st0", "st1"] + ["ld%d" % i for i in range(5)]
+              + ["ck%d" % t for t in range(RO)] + ["ay%d" % t for t in range(RO)]
               + ["ap%d%d" % (t, c) for t in range(RO) for c in range(2)])
 
 
@@ -67,285 +62,331 @@ def isap(a):
     return isinstance(a, tuple) and len(a) > 0 and a[0] in ("ap", "ind")
 
 
+def config(st):
+    over = {}
+    for t in range(RO):
+        for c in range(2):
+            over[(t, c)] = dict({"yr": "G", "bl": 1, "pn": "S", "bs": 0, "pp": 1},
+                                **dict(st["per"][c], **(st["r0"][c] if t == 0 else st["r3"][c] if t == RO - 1 else {})))
+    return dict(over=over, **st.get("x", {}))
+
+
 def program(cfg):
     ops = []
-    ch = cfg["ch"]
-    nc = len(ch)
-    base = [sum(ch[:c]) for c in range(nc)]
-    down = list(range(nc - 1, -1, -1))
+    n, m = CH, CH // 16
     at = [-1, 0]
 
     def op(q, ins, name):
-        ops.append({"q": q, "ins": ins if isinstance(ins, list) else [ins], "name": name + str(at[1]), "t": at[0]})
+        ops.append({"q": q, "ins": ins if isinstance(ins, list) else [ins], "name": name, "at": tuple(at)})
 
     def pick(kind):
-        return OPT[kind][int(cfg["pick"][(KINDS.index(kind) * RO + at[0]) * nc + at[1]], 16)]
+        return cfg["over"][(at[0], at[1])][kind]
+
+    def used(kind, q):
+        return any(q in v[kind] for v in cfg["over"].values())
 
     def pieces(kind):
+        s = pick(kind)
         out = []
-        for i, q in enumerate(pick(kind)):
+        for i, q in enumerate(s):
+            a, b = n * i // len(s), n * (i + 1) // len(s)
             if q == "+":
-                out[-1] = (out[-1][0], out[-1][1], 512 * i + 512)
+                out[-1] = (out[-1][0], out[-1][1], b)
             else:
-                out.append((q, 512 * i, 512 * i + 512))
+                out.append((q, a, b))
         return out
 
     def nm(o): return o[1] if o[0] == "ap" else "scat"
-    def tt(o, a, b, f, x=""): op("D", ("tt", o, a, b, f), nm(o) + x)
+    def tt(o, a, b, f): op("D", ("tt", o, a, b, f), nm(o))
     def ts(o, a, s1, s2, f0, f1=None): op("D", ("ts", o, a, s1, s2, f0, f1), nm(o))
     def act(o, a, f, b=0.0, s=1.0): op("A", ("act", o, a, f, b, s), nm(o))
     def cp(o, a, q="D"):
         if q == "D":
             op("D", ("cp", o, a), nm(o))
+        elif q == "G":
+            op("G", ("rep", o, a), nm(o))
         else:
             act(o, a, "Copy")
     def ms(o, v): op("D", ("ms", o, v), nm(o))
-    def mm(terms, name):
-        op("P", [("mm", o, l, r, i == 0, i == len(terms) - 1) for i, (o, l, r) in enumerate(terms)], name)
+    def mm(terms, name, first=True, last=True):
+        op("P", [("mm", o, l, r, first and i == 0, last and i == len(terms) - 1) for i, (o, l, r) in enumerate(terms)], name)
     def iota(o, pat, b, cm): op("G", ("iota", o, pat, b, cm), nm(o))
+    def row(name, k=128): return A(name, 0, k, 1, 0, 1)
+    def cs(i): return A("cs", i, i + 1)
 
-    op("A", ("dma", A("vt"), A("val", 0, W), "ld0"), "ldv")
     op("S", ("dma", A("ni"), A("nam", 0, R), "ld1"), "ldn")
-    op("S", ("dma", A("ys", 0, R), A("seen", 0, R), "ld2"), "lds")
-    op("S", ("dma", A("ki"), A("clk", 0, W), "ld3"), "ldk")
+    op("A", ("dma", A("ys", 0, R), A("seen", 0, R), "ld2"), "lds")
+    op("A", ("dma", A("vt"), A("val", 0, W), "ld0"), "ldv")
+    op("S", ("dma", A("ki", 0, W // 2), A("clk", 0, W // 2), "ld3"), "ldk")
+    op("S", ("dma", A("ki", W // 2, W), A("clk", W // 2, W), "ld4"), "ldk")
     iota(A("pj"), [[1, 16]], 0, 1)
     iota(A("col"), [[1, 144]], 0, 0)
-    iota(A("j16"), [[1, 32], [0, 16]], 0, 0)
     iota(A("colk"), [[0, 8], [1, 16]], 0, 0)
     iota(A("colg"), [[16, 8], [0, 16]], 0, 0)
     ts(A("pa"), A("pj"), 15, None, "bitwise_and")
-    ts(A("pb", 0, 1), A("pj", 0, 1), 31, None, "bitwise_and")
     cp(A("ka"), A("pa"))
     acol = A("ka", 0, 1)
-    tt(A("cs", 0, 1), A("pj", 0, 1), A("pa", 0, 1), "subtract")
-    g16 = A("cs", 0, 1)
-    cp(A("cs", 1, 2), A("pb", 0, 1))
+    tt(cs(0), A("pj", 0, 1), A("pa", 0, 1), "subtract")
+    g16 = cs(0)
     ts(A("cc"), A("ka"), g16, None, "add")
-    ts(A("cs", 2, 3), g16, 15.0, None, "add")
-    ts(A("cs", 3, 4), acol, -0.5, 0.5, "mult", "add")
-    ts(A("cs", 6, 7), acol, float(W), None, "add")
+    ts(cs(2), g16, 15.0, None, "add")
+    if used("sg", "A"):
+        ts(cs(3), acol, -1024.0, 1025.0 - W, "mult", "add")
+    if used("sg", "D"):
+        ts(cs(4), acol, 0.0, 1.0 - W, "mult", "add")
+    ts(cs(6), acol, float(W), None, "add")
     c128, me = A("col", 0, 128), A("cc", 0, 1)
     ts(A("idb"), c128, me, None, "is_equal")
     act(A("nid"), A("idb"), "Copy", 0.0, -1.0)
-    ts(A("e32"), A("j16"), A("cs", 1, 2), None, "is_equal")
     ts(A("be"), A("colg", 0, 128, 16), g16, 16.0, "is_equal", "mult")
-    act(A("one"), A("colk"), "Copy", 1.0, 0.0)
+    if used("re", "D"):
+        act(A("bf"), A("be"), "Copy", 0.0, 2.0)
+        act(A("bg"), A("be"), "Copy", 0.0, -1.0)
+    ms(row("one"), 1.0)
+    ms(row("neg"), -1.0)
+    ms(row("big"), 4096.0)
     ms(A("bigm"), 0.0)
     ms(A("bigm", 0, 128, 16), 1048576.0)
-    cp(A("bcm", 0, 8), A("col", 0, 8))
-    cp(A("bcm", 8, 12), A("col", 0, 8, 2))
-    ts(A("cs", 7, 8), acol, W + 16.0, None, "add")
-    act(A("ez"), A("colk"), "Relu", 1.0, -1.0)
+    ts(A("end"), A("col", 0, 8), 16.0, 15.0, "mult", "add")
+    act(row("ez"), row("colk"), "Relu", 1.0, -1.0)
     ts(A("blk"), A("colg"), g16, None, "is_equal")
+    act(A("bb"), A("blk"), "Copy", 0.0, 4096.0)
+    act(A("nbb"), A("blk"), "Copy", 0.0, -4096.0)
     act(A("idf"), A("idb"), "Copy")
     act(A("nst"), A("idb"), "Copy", 0.0, -16.0)
-    ts(A("tri"), A("colk"), acol, 8192.0, "is_le", "mult")
-    ts(A("gt"), A("colk"), acol, 0.5, "is_gt", "mult")
-    act(A("hid"), A("idb"), "Copy", 0.0, 0.5)
+    ts(A("gt"), A("colk"), acol, None, "is_gt")
     tt(A("gb"), A("gt"), A("blk"), "mult")
-    tt(A("lz"), A("hid"), A("gb"), "subtract")
+    tt(A("gt"), A("idb"), A("gb"), "subtract")
+    act(A("lz"), A("gt"), "Copy", 0.0, 1024.0)
     ts(A("rot"), c128, A("cc", 1, 2), None, "is_equal")
     ts(A("nri"), c128, A("cc", 15, 16), -1.0, "is_equal", "mult")
-    ts(A("zs"), A("col"), A("cs", 2, 3), None, "is_equal")
-    act(A("zb"), A("zs"), "Copy", 0.0, 4096.0)
-    iota(A("sm"), [[0, 64], [2048, 16]], 0, 0)
-    ts(A("nn"), A("col", 0, 8), 16.0, acol, "mult", "add")
-    ts(A("otc", 0, 8), A("nn"), 8192.0, None, "mult")
-    for c in down:
+    ts(A("zs"), A("col"), cs(2), None, "is_equal")
+    ms(A("sm"), 2048.0)
+    ms(A("sm", 0, 1024, 16), 0.0)
+    ts(A("wg"), A("col", 0, 16), acol, 4096.0, "is_lt", "mult")
+    ts(A("wh"), A("col", 0, 16), acol, 4096.0, "is_equal", "mult")
+    tt(A("wg"), A("wg"), A("wh"), "subtract")
+    for a in range(16):
+        o = A("dd", 128 * a, 128 * a + 128)
+        if cfg.get("dd", "DDDA")[a % 4] == "D":
+            ts(o, A("idb"), A("wg", a, a + 1), None, "mult")
+        else:
+            act(o, A("idb"), "Copy", 0.0, A("wg", a, a + 1))
+    if any(v["bl"] == 2 for v in cfg["over"].values()):
+        act(A("bid"), A("idb"), "Copy", 0.0, 4096.0)
+        op("D", ("ts", cs(7), acol, W + 16.0, None, "add", None), "c7")
+    ts(A("p4", 0, 1), A("pj", 0, 1), 3, None, "bitwise_and")
+    for kv in sorted(set(4 * v["cm"].count("D") for v in cfg["over"].values())):
+        i = 8 + kv // 2
+        ts(cs(i), A("p4", 0, 1), float(kv // 4), 4.5, "is_lt", "mult")
+        ts(cs(i), cs(i), 7.0, None, "add")
+        if used("sg", "A"):
+            ts(cs(i + 1), cs(i), -1.0, None, "mult")
+    for c in range(2):
         ms(A("st", 144 * c, 144 * c + 16), 1.0)
-    ms(A("kt", W, W + 32), 0.0)
-    ms(A("kt", 2 * W + 32, 2 * W + 64), 0.0)
-    for h in (1, 0):
-        cp(A("pu", 128 * h, 128 * h + 128), A("ni", 128 * h, 128 * h + 128))
-        mm([(A("ps%d" % h, 0, 128), A("ys", 128 * h, 128 * h + 128), A("idb"))], "yT")
-        cp(A("yt", 128 * h, 128 * h + 128), A("ps%d" % h, 0, 128), "A")
-    act(A("bf"), A("be"), "Copy", 0.0, 2.0)
-    act(A("bg"), A("be"), "Copy", 0.0, -1.0)
-    for t in range(1, RO):
-        ways = set()
-        for c in down:
-            at[:] = [t, c]
-            ways.add(pick("vm"))
-        at[:] = [-1, 0]
-        if 0 in ways:
-            op("G", ("rdma", A("yt", t * R, t * R + R), A("yt", 0, R), HOP * t, "ay%d" % t), "sendy")
-        if 1 in ways:
-            op("G", ("rdma", A("ys", t * R, t * R + R), A("ys", 0, R), HOP * t, "az%d" % t), "sendy")
-    cp(A("kt", 0, 1024), A("ki", 0, 1024))
-    cp(A("kt", 1024, W), A("ki", 1024, W))
+    if used("pn", "D") or used("pn", "A"):
+        ms(A("pn"), 0.0)
+    for k0 in (0, TW):
+        ms(A("kt", k0, k0 + PAD), 0.0)
+        ms(A("kt", k0 + PAD + W, k0 + TW), 0.0)
+    ts(A("pb", 0, 1), A("pj", 0, 1), 31, None, "bitwise_and")
+    ts(cs(1), A("pb", 0, 1), 16.0, None, "mult")
+    for j in range(4):
+        ts(A("e32", 128 * j, 128 * j + 128), A("colg"), 128.0 * j, cs(1), "add", "is_equal")
+    mm([(A("ps0", 128 * h, 128 * h + 128), A("ys", 128 * h, 128 * h + 128), A("idb")) for h in (1, 0)], "yT")
+    cp(A("ys", R, 2 * R), A("ps0", 0, R), "A")
+    op("G", ("rdma", A("ys", 2 * R, 3 * R), A("ys", 0, R), HOP, "ay1"), "sendy")
+    op("G", ("rdma", A("ys", 3 * R, 4 * R), A("ys", R, 2 * R), HOP, "ay0"), "sendy")
+    for t in range(2, RO):
+        op("G", ("rdma", A("ys", 2 * R * t, 2 * R * t + 2 * R), A("ys", 0, 2 * R), HOP * t, "ay%d" % t), "sendy")
+    for h in range(2):
+        cp(A("kt", PAD + 1024 * h, PAD + 1024 * h + 1024), A("ki", 1024 * h, 1024 * h + 1024), cfg.get("kc", "DD")[h])
 
     def sel(a): return A("zs", 15 - a, 143 - a)
-    def big(a): return A("zb", 15 - a, 143 - a)
     wide = [0]
 
     def turn():
         wide[0] += 1
-        return A("ps%d" % (1 - wide[0] % 2))
-
-    def chunk(c):
-        def B(name, a=0, b=None, step=1, p1=128):
-            w, o = (PER[name][0] * ch[c], PER[name][0] * base[c]) if name in PER else (SLOT[name][0], SLOT[name][0] * c)
-            return A(name, o + a, o + (w if b is None else b), step, 0, p1)
-        return B
+        return "ps%d" % (wide[0] % NWIDE)
 
     for t in range(RO):
         at[:] = [t, 0]
-        k0, k1 = (W + 32) * (t % 2), (W + 32) * (1 - t % 2)
-        KT = A("kt", k0, k0 + W)
-        op("S", ("dma", A("kt", k1, k1 + W), KT, "ck%d" % t), "cpk")
-        for c in down:
+        k0, k1 = TW * (t % 2), TW * (1 - t % 2)
+        KT = A("kt", k0 + PAD, k0 + PAD + W)
+        op("S", ("dma", A("kt", k1 + PAD, k1 + PAD + W), KT, "ck%d" % t), "cpk")
+        runs = []
+        for c in (1, 0):
             at[:] = [t, c]
-            n, m, B = ch[c], ch[c] // 16, chunk(c)
-            x = n // 2 if cfg["bl"] == 2 else 0
-            def S(name, a=0, b=n, step=1, p1=128):
-                return A("ps%d" % (2 + 3 * c + TILE[name][0]), TILE[name][1] + a, TILE[name][1] + b, step, 0, p1)
-            ksp, orep, pps, om2, cnt, zz, p1p, bak = (S(k) for k in ("ksp", "orep", "pps", "om2", "cnt", "zz", "p1p", "bak"))
-            key, oot, dup = S("key", 0, 128), S("oot", 0, m), S("dup", 0, m)
-            pc = t * R + base[c]
-            def PU(a, b): return A("pu", pc + a // 16, pc + b // 16)
-            PF = B("pf")
-            cp(PF, A("pu", pc, pc + n))
-            flat = pick("vm")
-            both = flat and "D" in pick("re")
-            for k in range(16 if flat else 0):
-                op("G", ("rep", A("yr", 16 * pc + k, 16 * (pc + n), 16), A("ys", pc, pc + n)), "yr")
-            for q, a, b in pieces("re") if flat else []:
-                tt(B("vg", a, b), IND(A("vt"), PU(a, b)), A("yr", 16 * pc + a, 16 * pc + b), "subtract")
-                if q == "A":
-                    act(B("ab", a, b), B("vg", a, b), "Relu" if both else "Abs")
+            for q, a, b in pieces("vg")[::-1]:
+                if q != "D":
+                    continue
+                lo, hi = n * c + a, n * c + b
+                if runs and runs[-1][0] == pick("yr") and runs[-1][1] == hi and (pick("yr") == "G" or b < n):
+                    runs[-1] = (pick("yr"), lo, runs[-1][2])
                 else:
-                    ts(B("ab", a, b), B("vg", a, b), 0.0, None, "max")
-            for q, a, b in [] if flat else pieces("vg"):
-                cp(B("vg", a, b), IND(A("vt"), PU(a, b)), q)
-            for q in range(0 if flat else n // 32):
-                wb = turn()
-                u = base[c] // 32 + q
-                y0, p0 = t * R + 128 * (u // 4), 32 * (u % 4)
-                mm([(wb, A("yt", y0, y0 + 128, 1, p0, p0 + 32), A("e32", 0, 512, 1, p0, p0 + 32)),
-                    (wb, A("nid"), B("vg", 512 * q, 512 * q + 512))], "diff")
-                act(B("ab", 512 * q, 512 * q + 512), wb, "Abs")
-            mm([(key, A("one", 0, 128, 1, 0, 1), A("colk", 0, 128, 1, 0, 1))]
-               + [(S("key", k, 128, 16, n), B("vg", k, 16 * n, 16), A("bg")) for k in range(16 if both else 0)]
-               + [(S("key", k, 128, 16, n), B("ab", k, 16 * n, 16), A("bf" if both else "be")) for k in range(16)], "key")
-            op("D", ("scan", B("pm"), A("bigm"), key, 0.0, "add", "min"), "pm")
-            cp(B("mn"), B("pm", 15, 128, 16))
-            tt(B("st", 16, 144), IND(B("mn"), A("bcm", 0, 8)), B("pm"), "is_equal")
-            mm([(ksp, B("st", 16, 144, 1, n), A("idb", 0, n, 1, 0, n)), (ksp, B("st", 15, 143, 1, n), A("nid", 0, n, 1, 0, n)),
-                (ksp, A("ez", 0, 128, 1, 0, 1), A("one", 0, n, 1, 0, 1))], "ksp")
-            tt(B("xo"), ksp, PF, "mult")
-            mm([(orep, A("blk"), B("xo"))], "orep")
-            fused = pick("cm")[0] == "D"
-            mm([(oot, sel(a), B("xo", a, n, 16)) for a in range(16)], "oot")
-            if fused:
-                op("D", ("cp", B("ou"), orep), "ou")
+                    runs.append((pick("yr"), lo, hi))
+        for q, lo, hi in runs:
+            at[:] = [t, int(hi > n)]
+            for k in range(16):
+                cp(A("yr", 16 * (t * R + lo) + k, 16 * (t * R + hi), 16), A("ys", 2 * R * t + lo, 2 * R * t + hi), q)
+        for c in (1, 0):
+            at[:] = [t, c]
+            def B(name, a=0, b=None, step=1):
+                w = PER[name][0] * n if name in PER else SLOT[name][0]
+                return A(name, w * c + a, w * c + (w if b is None else b), step)
+            def S(name, a=0, b=n, step=1):
+                return A("ps%d" % (NWIDE + 2 * c + TILE[name][0]), TILE[name][1] + a, TILE[name][1] + b, step)
+            key, ksp, orep, pps, cnt, zz, p1p, bak, jpp, x = (
+                S(k) for k in ("key", "ksp", "orep", "pps", "cnt", "zz", "p1p", "bak", "jpp", "x"))
+            oot, otp, dup = S("oot", 0, m), S("otp", 0, m), S("dup", 0, m)
+            pc = t * R + n * c
+            PF = A("pf", pc, pc + n)
+            def PU(a, b): return A("pu", n * c + a, n * c + b)
+            if t == 0:
+                cp(PU(0, n), A("ni", pc, pc + n))
+                cp(PF, A("ni", pc, pc + n))
             else:
-                op("D", ("cp", B("oo", 0, m), oot), "ou")
-                cp(B("ko"), IND(KT, B("oo", 0, m)), pick("ko"))
-                mm([(S("kop", 0, 128, 1, n), B("ko"), A("idb"))], "kop")
-                cp(B("kq", 0, 128, 1, n), S("kop", 0, 128, 1, n), pick("kq"))
+                cp(PU(0, n), PF)
+            if pick("pp"):
+                mm([(pps, A("idb"), PF)], "pps")
+            head = [(key, row("one"), row("colk"))]
+            both = "D" in pick("re")
+            runs = []
+            for (q, a, b), r in zip(pieces("vg"), pick("re")):
+                vg = B("vg", 16 * a, 16 * b)
+                if q == "D":
+                    tt(vg, IND(A("vt"), PU(a, b)), A("yr", 16 * (pc + a), 16 * (pc + b)), "subtract")
+                    if r == "+" and runs[-1][3] is None:
+                        runs[-1][2] = b
+                        continue
+                    src = None
+                else:
+                    cp(vg, IND(A("vt"), PU(a, b)), q.upper())
+                    src = A(turn())
+                    y0 = 2 * R * t + R + n * c
+                    mm([(src, A("ys", y0, y0 + 128, 1, a, a + 32), A("e32", 0, 512, 1, a, a + 32)), (src, A("nid"), vg)], "dv")
+                runs.append([runs[-1][0] if r == "+" else r, a, b, src])
+            for r, a, b, src in runs:
+                ab = B("ab", 16 * a, 16 * b)
+                src, sign = (src, -1.0) if src else (B("vg", 16 * a, 16 * b), 1.0)
+                if r == "A":
+                    act(ab, src, "Relu" if both else "Abs", 0.0, sign)
+                else:
+                    ts(ab, src, sign, 0.0, "mult", "max")
+            if both:
+                mm(head + [(S("key", k, 128, 16), B("vg", k, 16 * n, 16), A("bg")) for k in range(16)], "key", True, False)
+            mm(([] if both else head)
+               + [(S("key", k, 128, 16), B("ab", k, 16 * n, 16), A("bf" if both else "be")) for k in range(16)],
+               "key", not both, True)
+            op("D", [("scan", B(u), A("bigm"), key, 0.0, "add", "min") for u in ("pm", "pn")[:1 + (pick("pn") == "S")]], "pm")
+            if pick("pn") != "S":
+                cp(B("pn", 15, 128, 16), B("pm", 15, 128, 16), pick("pn"))
+            tt(B("st", 16, 144), IND(B("pn"), A("end")), B("pm"), "is_equal")
+            mm([(ksp, row("ez"), row("one")), (ksp, B("st", 16, 144), A("idb")), (ksp, B("st", 15, 143), A("nid"))], "ksp")
+            tt(B("xo"), ksp, PF, "mult")
+            mm([(oot, sel(a), B("xo", a, n, 16)) for a in range(16)], "oot")
+            cp(B("oo"), oot)
+            cp(B("ko"), IND(KT, B("oo")), pick("ko"))
             cp(B("ks"), ksp, pick("ks"))
+            cp(B("o3"), oot, pick("o3"))
             if pick("eq") == "D":
+                mm([(orep, A("blk"), B("xo"))], "orep")
                 tt(B("eq"), orep, PF, "is_equal")
             else:
-                mm([(zz, A("nid"), PF), (zz, A("blk"), B("xo"))], "eqp")
-                act(B("ne"), zz, "Abs")
+                mm([(orep, A("nid"), PF), (orep, A("blk"), B("xo"))], "orep")
+                act(B("ne"), orep, "Abs")
                 act(B("eq"), B("ne"), "Relu", 1.0, -1.0)
-            mm([(om2, A("idb"), A("tri", 0, n)), (om2, A("blk"), B("xo"))]
-               + [(S("om2", n + 16 * j, n + 16 * j + 16), A("blk"), B("xo", 32 * j + 16, 32 * j + 32)) for j in range(x // 16)], "omp")
-            cp(B("om", 0, n + x), S("om2", 0, n + x), pick("om"))
-            tt(B("od", 0, m), oot, A("otc", 0, m), "subtract")
-            mm([(pps, A("idb"), PF)], "pps")
+            kv = 4 * pick("cm").count("D")
+            if kv:
+                kop = turn()
+                mm([(A(kop, j, 4 * n, 4), A("idb"), B("ko")) for j in range(4)], "kop")
+            pairs = [(S("x", n + 16 * j, n + 16 * j + 16), 32 * j) for j in range(m // 2 if pick("bl") == 2 else 0)]
+            mm([(x, A("blk"), B("xo"))] + [(o, A("blk"), B("xo", a, a + 16)) for o, a in pairs]
+               + [(S("x", a, n, 16), A("nid"), B("o3")) for a in range(16)]
+               + [(S("x", n + a, n + 64, 16), A("nid"), B("o3", 1, m, 2)) for a in range(16 if pairs else 0)], "x", True, False)
             for q, a, b in pieces("kg"):
-                cp(B("kg", a, b), IND(KT, PU(a, b)), q)
-            for q, a, b in pieces("sj"):
+                cp(B("kg", 16 * a, 16 * b), IND(KT, PU(a, b)), q)
+            for j in range(pick("sj")):
+                a, b = 16 * n * j // pick("sj"), 16 * n * (j + 1) // pick("sj")
                 op("D", ("scan", B("js", a, b), A("sm", 0, b - a), B("kg", a, b), 0.0, "min", "max"), "js")
-            if pick("na") == "D":
-                tt(B("nw", 0, 2 * n, 2), pps, B("js", 15, 16 * n, 16), "max", "a")
-            else:
-                mm([(bak, A("nid"), PF), (bak, A("idb"), B("js", 15, 16 * n, 16))], "nwa")
-                act(B("rj"), bak, "Relu")
-                mm([(bak, A("idb"), PF), (bak, A("idb"), B("rj"))], "nwa")
-                op("A", ("act", B("nw", 0, 2 * n, 2), bak, "Copy", 0.0, 1.0), "nwa")
-            for q, a, b in pieces("cm"):
-                if fused:
-                    tt(B("cm", a, b), IND(KT, B("ou", a // 16, b // 16)), B("kg", a, b), "is_le")
-                    continue
-                wb = turn()
-                p0 = a // 16
-                mm([(wb, ("ap", "kq", p0, p0 + 32, 128 * c, 128 * c + 128, 1), A("e32", 0, 512, 1, p0, p0 + 32)),
-                    (wb, A("nid"), B("kg", a, b))], "dik")
-                if q == "a":
-                    act(B("cm", a, b), wb, "Sign", 0.5, -1.0)
+            tt(B("mx"), pps if pick("pp") else PF, B("js", 15, 16 * n, 16), "max")
+            runs = [int(k) for k in {0: "0123", 4: "1023", 8: "0213", 12: "0312", 16: "0123"}[kv]]
+            for u in runs:
+                a, b = 4 * u, 4 * u + 4
+                if a < kv:
+                    tt(B("cm", n * a, n * b), B("kg", u, 16 * n, 4), A(kop), "is_ge")
                 else:
-                    ts(B("cm", a, b), wb, 0.0, 2.0, "is_le", "mult")
-            for a in range(0, n, 64):
-                b = min(n, a + 64)
-                o = S("cnt", a, b)
-                fix = [(S("cnt", u, u + 32), A("nst"), A("one", 0, 32)) for u in range(a, b, 32) if pick("cm")[u // 32] == "d"]
-                mm([(o, A("nst"), B("eq", a, b))] + fix
-                   + [(o, sel(k), B("cm", 16 * a + k, 16 * b, 16)) for k in range(16)], "cnt")
+                    wb = turn()
+                    mm([(A(wb), A("idb"), B("kg", u, 16 * n, 4))], "dk", True, False)
+                    mm([(A(wb, j, 4 * n, 4), A("nid"), B("ko")) for j in range(4)], "do", False, True)
+                    act(B("cm", n * a, n * b), A(wb), "Sign", 0.5, 1.0)
+                terms = [(cnt, sel(u + 4 * j), B("cm", n * a + j, n * b, 4)) for j in range(4)]
+                mm(([(cnt, A("nst"), B("eq"))] if u == runs[2] else []) + terms, "cnt", u == runs[0], u == runs[3])
             if pick("sg") == "A":
-                act(B("sg"), cnt, "Sign", -11.5 if fused else -7.0, 1.0)
-                hb = A("cs", 3, 4)
+                act(B("sg"), cnt, "Sign", cs(9 + kv // 2), 1.0)
             else:
-                ts(B("sg"), cnt, 11.5 if fused else 7.0, 2.0, "is_ge", "mult")
-                hb = 0.0
-            mm([(zz, A("lz"), B("sg"))], "zz")
-            if pick("fi") == "A":
-                act(B("xb", 0, n), zz, "Relu", hb, 1.0)
+                ts(B("sg"), cnt, cs(8 + kv // 2), 2.0, "is_ge", "mult")
+            mm([(zz, A("idb"), PF), (zz, A("lz"), B("sg"))], "zz")
+            hb = cs(3 if pick("sg") == "A" else 4)
+            if pick("r") == "A":
+                act(B("r"), zz, "Relu", hb, 1.0)
             else:
-                ts(B("xb", 0, n), zz, hb, 0.0, "add", "max")
-            o1, o2, otp = S("otp", 0, m), S("otp", m, 2 * m), S("otp", 0, 2 * m)
-            first = (o1, A("idb"), A("otc", 0, m))
-            if pick("so"):
-                mm([first] + [(o1, big(a), B("xb", a, n, 16)) for a in range(16)], "otp")
-                tt(B("ta", 0, m), o1, B("od", 0, m), "add")
-            tt(B("xb", n, 2 * n), pps, B("xb", 0, n), "mult", "p")
-            if pick("so"):
-                mm([(o2, big(a), B("xb", n + a, 2 * n, 16)) for a in range(16)], "otp")
-            else:
-                mm([first, (o2, A("idb"), A("bigm", 1, 1 + m))]
-                   + [(otp, big(a), B("xb", a, 2 * n, 16)) for a in range(16)], "otp")
-                tt(B("ta", 0, m), o1, B("od", 0, m), "add")
-            mm([(p1p, A("nri"), PF), (p1p, A("blk"), B("xb", n, 2 * n))], "ppp")
-            ts(B("ot", 0, 2 * m), otp, 1.0 / 4096, None, "mult")
+                ts(B("r"), zz, hb, 0.0, "add", "max")
+            mm([(otp, sel(a), B("r", a, n, 16)) for a in range(16)], "otp")
+            ts(B("ot"), otp, PAD - 1.0, None, "add")
+            mm([(p1p, row("neg"), row("one")), (p1p, A("nri"), PF), (p1p, A("blk"), B("r"))], "p1p")
             tt(B("tp"), p1p, B("ks"), "mult")
-            tt(B("kf"), IND(KT, B("ot", m, 2 * m)), B("ks"), "mult")
-            mm([(bak, A("idb"), PF), (bak, A("nid"), B("xo")), (bak, A("rot"), B("tp")), (bak, A("idb"), B("kf"))], "bak")
-            cp(B("nw", 1, 2 * n, 2), bak, pick("nw"))
-            if t < RO - 1:
-                src, dst, hop = A("po", pc, pc + n), A("pu", pc + R, pc + R + n), HOP
+            if pick("jp") == "A":
+                mm([(jpp, A("idb"), B("mx")), (jpp, A("nbb"), B("r"))], "jpp")
+                act(B("jp"), jpp, "Relu")
             else:
-                src, dst, hop = A("pl", base[c], base[c] + n), A("ph", base[c], base[c] + n), -HOP * t
-            op("D", ("cp", src, IND(B("nw"), B("ot", 0, m))), "po")
+                mm([(jpp, row("big"), row("one")), (jpp, A("nbb"), B("r"))], "jpp")
+                tt(B("jp"), jpp, B("mx"), "min")
+            tt(B("kf"), IND(A("kt", k0, k0 + PAD + W), B("ot")), B("ks"), "mult")
+            terms = [(bak, A("idb"), PF), (bak, A("nid"), B("xo")), (bak, A("rot"), B("tp")), (bak, A("idb"), B("kf"))]
+            if pick("bs"):
+                mm(terms[:3], "bah", True, False)
+            mm(terms[3 * pick("bs"):], "bak", not pick("bs"), True)
+            if t < RO - 1:
+                src, dst, hop = A("po", pc, pc + n), A("pf", pc + R, pc + R + n), HOP
+            else:
+                src, dst, hop = A("pl", n * c, n * c + n), A("ph", n * c, n * c + n), -HOP * t
+            tt(src, bak, B("jp"), "max")
             op("G", ("rdma", dst, src, hop, "ap%d%d" % (t, c)), "sendp")
             if t == RO - 1:
-                op("S", ("dma", A("yp", base[c], base[c] + n), dst, "st%d" % c), "stp")
-            tt(B("ea", 0, n + x), IND(B("ta", 0, m), A("bcm", 0, m + x // 16)), B("om", 0, n + x), "is_equal")
-            mm([(dup, A("idf"), B("ta", 0, m))] + [(dup, big(a), B("ea", a, n, 16)) for a in range(16)]
-               + [(S("dup", 1, m, 2), big(a), B("ea", n + a, n + x, 16)) for a in range(16 if x else 0)], "dup")
-            if x:
-                for j in range(2):
-                    ts(B("of", j, m, 2), S("dup", j, m, 2), A("cs", 6 + j, 7 + j), None, "min")
+                op("S", ("dma", A("yp", n * c, n * c + n), dst, "st%d" % c), "stp")
+            mm([(x, A("bb"), B("r"))] + [(o, A("bb"), B("r", a, a + 16)) for o, a in pairs], "x", False, True)
+            xw = n + 16 * len(pairs)
+            if pick("ea") == "D":
+                ts(B("ea", 0, xw), S("x", 0, xw), 0.0, None, "is_equal")
             else:
-                ts(B("of", 0, 2 * m, 2), dup, A("cs", 6, 7), None, "min")
-        for c in down:
-            at[:] = [t, c]
-            B = chunk(c)
-            u = cfg["bl"]
-            for m in range(ch[c] // (16 * u) - 1, -1, -1):
-                cp(IND(A("kt", k1, k1 + W + 32), B("of", 2 * m, 2 * m + u)), B("js", 256 * u * m + 15, 256 * u * (m + 1), 16))
+                act(B("nf", 0, xw), S("x", 0, xw), "Abs")
+                act(B("ea", 0, xw), B("nf", 0, xw), "Relu", 1.0, -1.0)
+            mm([(dup, row("big"), row("one", m)), (dup, A("idb"), B("o3"))]
+               + [(dup, A("dd", 128 * a, 128 * a + 128), B("ea", a, n, 16)) for a in range(16)]
+               + [(S("dup", 1, m, 2), A("bid"), B("ea", n + a, xw, 16)) for a in range(16 if pairs else 0)], "dup")
+            if pairs:
+                op("D", [("ts", B("of", j, m, 2), S("dup", j, m, 2), cs(6 + j), None, "min", None) for j in range(2)], "of")
+            else:
+                ts(B("of", 0, 2 * m, 2), dup, cs(6), None, "min")
+            u = pick("bl")
+            for b in range(m // u - 1, -1, -1):
+                cp(IND(A("kt", k1 + PAD, k1 + TW), B("of", 2 * b, 2 * b + u)), B("js", 256 * u * b + 15, 256 * u * (b + 1), 16))
+    at[:] = [RO, 0]
+    def kcol(b, e): return A("kt", PAD + 256 * b, PAD + 256 * e)
     fo = A("ps0", 0, 256)
-    mm([(fo, A("idf"), A("kt", 256 * b, 256 * b + 256)) for b in range(4)], "fold")
-    tt(A("fa"), A("kt", 1024, 1536), A("kt", 1536, 2048), "add")
-    tt(A("fb"), A("fa", 0, 256), A("fa", 256, 512), "add")
-    tt(A("fc"), fo, A("fb"), "add")
+    mm([(fo, A("idf"), kcol(0, 1))], "fold", True, False)
+    runs = [("A", 1, 3), ("D", 4, 6), ("A", 3, 4), ("D", 6, 8)]
+    for q, a, b in runs:
+        cp(A("fh", 256 * a, 256 * b), kcol(a, b), q)
+        mm([(fo, A("idb"), A("fh", 256 * j, 256 * j + 256)) for j in range(a, b)], "fold", False, b == 8)
+    cp(A("fc"), fo, "A")
     op("S", ("dma", A("yk", 0, 256), A("fc"), "stk"), "stk")
     return ops
 
 
 def links(ops):
-    hist = {}
+    hist, lastp = {}, {}
     for x, o in enumerate(ops):
         wr, rd = set(), set()
         for i in o["ins"]:
@@ -356,13 +397,18 @@ def links(ops):
                 (rd if n else wr).add((a[1], a[4], a[5]))
         o["banks"] = sorted(set(r[0] for r in wr | rd if r[0].startswith("ps")))
         o["dma"] = o["ins"][0][0] in ("dma", "rdma")
-        dep = {}
+        dep = set()
         for regs, mine in ((rd, False), (wr, True)):
             for nm, lo, hi in regs:
                 for y, l2, h2, w2 in hist.get(nm, []):
                     if l2 < hi and lo < h2 and (mine or w2) and not (nm == "yr" and mine):
-                        dep[y] = dep.get(y, False) or (w2 and not mine)
-        o["dep"] = dep
+                        dep.add(y)
+        if o["q"] == "P":
+            for b in o["banks"]:
+                if b in lastp:
+                    dep.add(lastp[b])
+                lastp[b] = x
+        o["dep"] = sorted(dep)
         for regs, mine in ((rd, False), (wr, True)):
             for nm, lo, hi in sorted(regs):
                 h = hist.setdefault(nm, [])
@@ -371,36 +417,67 @@ def links(ops):
                 h.append((x, lo, hi, mine))
 
 
-def plan(cfg):
-    ops = program(cfg)
+def waits(ops, o, last):
+    q = o["q"]
+    wait = [y for y in o["dep"] if ops[y]["q"] != q or q != "P"]
+    for b in o["banks"]:
+        wait += [y for q2, y in last.get(b, {}).items() if q2 != q]
+    return wait
+
+
+AL = "0123456789abcdefghijklmnopqrstuvwxyzABCDEFGHIJKLMNOPQRSTUVWXYZ"
+
+
+def order_of(ops, st):
+    keys, cnt = [], {}
+    for o in ops:
+        t, c = o["at"]
+        i = cnt.get((o["name"], t, c), 0)
+        cnt[(o["name"], t, c)] = i + 1
+        keys.append(("0" if t <= 0 else "e" if t >= RO else "") + o["name"] + "0123456789ABCDEFGHIJKLMNOPQRSTUVWXYZ"[i]
+                    + ("ba"[c] if 0 <= t < RO else ""))
+    z = st["phi"]
+    phi = {k: (AL.index(z[3 * i]) * 3844 + AL.index(z[3 * i + 1]) * 62 + AL.index(z[3 * i + 2])) * 2.0
+           for i, k in enumerate(sorted(set(keys)))}
+    rank = [phi[k] + (o["at"][0] - 2) * st["T"] * (0 < o["at"][0] < RO) for k, o in zip(keys, ops)]
+    seq, done = [], set()
+    todo = sorted(range(len(ops)), key=lambda x: (rank[x], x))
+    while todo:
+        x = next(x for x in todo if all(y in done for y in ops[x]["dep"]))
+        todo.remove(x)
+        done.add(x)
+        seq.append(x)
+    return seq
+
+
+def plan(st):
+    ops = program(config(st))
     links(ops)
-    al = "0123456789abcdefghijklmnopqrstuvwxyzABCDEFGHIJKLMNOPQRSTUVWXYZ"
-    s = cfg["seq"]
     order = {q: [] for q in "DAPGS"}
     total = {q: 0 for q in "DAPG"}
     seen = {q: {} for q in order}
     last = {}
-    for x in [al.index(s[i]) * 62 + al.index(s[i + 1]) for i in range(0, len(s), 2)]:
+    for i, x in enumerate(order_of(ops, st)):
         o = ops[x]
         q = o["q"]
-        wait = [y for y, raw in o["dep"].items() if raw or ops[y]["q"] != q or q != "P"]
+        o["pos"] = i
+        wait = waits(ops, o, last)
         for b in o["banks"]:
-            wait += [y for q2, y in last.get(b, {}).items() if q2 != q]
             last.setdefault(b, {})[q] = x
-        need = {}
-        for y in wait:
+        o["need"] = []
+        for y in sorted(set(wait), key=lambda y: -ops[y]["pos"]):
             sem, v = ops[y]["sig"]
             if v > seen[q].get(sem, 0):
-                need[sem] = max(v, need.get(sem, 0))
-        seen[q].update(need)
-        o["need"] = sorted(need.items())
+                o["need"].append((sem, v))
+                for s, u in ops[y]["knows"].items():
+                    seen[q][s] = max(u, seen[q].get(s, 0))
         if not o["dma"]:
             total[q] += 1
             o["sig"] = ("s" + q, total[q])
         else:
             o["sig"] = (o["ins"][0][3], 16) if o["ins"][0][0] == "dma" else (o["ins"][0][4], 1)
+        o["knows"] = dict({} if o["ins"][0][0] == "rdma" else seen[q], **{o["sig"][0]: o["sig"][1]})
         order[q].append(x)
-    assert sum(len(v) for v in order.values()) == len(ops)
     return ops, order, total
 
 
@@ -412,12 +489,12 @@ def rank_program(g, core, T, topo):
     if rank is None:
         return
     if "plan" not in MEMO:
-        MEMO["plan"] = plan(CFG)
+        MEMO["plan"] = plan(ST)
     ops, order, total = MEMO["plan"]
     cores = T.cores
     queue = {"D": g.vector, "A": g.scalar, "P": g.tensor, "G": g, "S": g.sync}
     alu = {"add": AluOpType.add, "subtract": AluOpType.subtract, "mult": AluOpType.mult, "max": AluOpType.max,
-           "min": AluOpType.min, "is_equal": AluOpType.is_equal, "is_le": AluOpType.is_le, "is_gt": AluOpType.is_gt,
+           "min": AluOpType.min, "is_equal": AluOpType.is_equal, "is_lt": AluOpType.is_lt, "is_gt": AluOpType.is_gt,
            "is_ge": AluOpType.is_ge, "bitwise_and": AluOpType.bitwise_and}
     fn = {"Copy": ActivationFunctionType.Copy, "Abs": ActivationFunctionType.Abs, "Sign": ActivationFunctionType.Sign,
           "Relu": ActivationFunctionType.Relu}
@@ -471,7 +548,7 @@ def rank_program(g, core, T, topo):
                     h = e.memset(a[0], a[1])
                 elif k == "act":
                     h = e.activation(a[0], a[1], fn[a[2]], bias=a[3], scale=a[4])
-                elif SCRATCH[i[1][1]][2] == "int32":
+                elif SCRATCH[i[1][1]][2] == I32:
                     h = e.iota(a[0], a[1], a[2], a[3])
                 else:
                     h = e.iota(a[0], a[1], a[2], a[3], allow_small_or_imprecise_dtypes=True)

from concourse.mybir import AluOpType, ActivationFunctionType

W, R, RO, HOP, NR = 2048, 256, 4, 3, 8
PAD, SPARE = 8, 32
TW = PAD + W + SPARE
H, BF, F, U16, I32 = "float16", "bfloat16", "float32", "uint16", "int32"
CH = 128

ST = {'per': [{'vg':'A+D+D+D+','re':'AAAAAAAA','kg':'A+A+A+D+','cm':'DDAA','sj': 2,'ko':'A','ks':'A','eq':'A','sg':'A','r':'A','jp':'D','o3':'D','ea':'D','bl': 1,'pn':'S','bs': 0,'pp': 1},{'vg':'D+D+A+A+','re':'A+A+A+A+','kg':'A+++A+++','cm':'DDAA','sj': 2,'ko':'D','ks':'A','eq':'A','sg':'D','r':'A','jp':'A','o3':'D','ea':'D','bl': 1,'pn':'S','pp': 1,'bs': 0}],'r0': [{'yr':'G','re':'AA+A+A+A','sj': 2,'ko':'D','sg':'A','ks':'A','ea':'A','r':'A','o3':'A','eq':'D','jp':'A','cm':'DDAA','kg':'A+++A+D+','vg':'A+d+d+d+','bl': 2,'pn':'S','pp': 0,'bs': 0},{'yr':'A','ko':'D','r':'D','ea':'A','eq':'D','ks':'A','kg':'A+A+A+A+','sg':'A','vg':'d+d+A+A+','jp':'D','o3':'D','sj': 2,'cm':'DDAA','bl': 1,'pn':'S','re':'A+A+A+A+','pp': 0}],'r3': [{},{}],'x': {'kc':'GD'},'T': 17400,'phi':'4lR4Sk4pH4Zz4mf50b4as56O5Ki6UE4Fm4mG3pp2uA3ZQ4y53eE3kq2XW52o5Os4Fw5Tm52661E4Il5Ws55y5YZ54J60s4Qi5N059V6212ts2B12yU3Mo2ui4yT37k5Gx4Gu4p34GV57I2AI3qS3Rj3bX3kK3Gy4tA3DJ2Su3II3l24wz3903YP3Xi4Sb2PM4UP5FP4YY5K24VK5Fi4UM5Pp6507hJ4au3WE4e651D4lJ4Dd4jP53S3Tg3bP41v49A5MK6JD3bA53b5xN33w3Gp2WQ4sg38g2Yj5Ke70S5D86b155o6985s264w2we42X58r5MO6xp4Pv57z4Ic5q94Pw57t4Id4Tp5Fh4Tn5zn5mC5zq4jf5gN2v94D62Cs4u33Kr4Cn08j08o08408908e57K5Go5V84i63em5se6HL3OF4MC3cp56N6906dk7lP2vs4Tx5xp4gF5lF4Tf5Bb5Hb6nG5Bu6bG5D46c23HZ2r32tt4td5gu2ml4Gl4Uw5XP7h23Jv3l85qF6bR4P26c36oM6n173U6sG5OB6S06Oo6K079O7hc7mJ6eQ6hw2KC40s3LN3Wx5c862m2hl3WL4W24E759A3dL5Kf6y04mF4wy4kt51t4gd50t4f84nN2Hw2Au2LJ58y69o5DA6474IR57A2J82Wb4GQ5iu68N9wqa4w8Dwa4L9es9Iua4xauRbJq9WPaqA9ZwaYi9Y1aKXa2iawva40b2Ha5Ya6x9itaEL9uYaOF8xl9TeaJ19V7b0m9Sx9tT9uaai4a70bwa9DYa3o8v2ak1b3cehXec3ej3erpejjernenveijecMe5x9YmaHYeeJawmbxwa8vbuM9ZjayRa7MaoA9oma77anYbse9Tqak89TPanAaxiaLr9E3a0T9TpaJjafuaGz94yatLaa2ax99Xoakk9BWaGxas7bEY9BraGt93Qa8h9IvaxRabOaZna6WaFbajhaz4aG5bJ38SCanyaFpbMs9E19Lw8sE9E2a5BabIatFbIIaVNbJbaxCbQNauibPtaUabNfbqBbSvbtdbAdbDxbtzb8Bby59SQbaO8ASapxaX2cpSaswbxv8DN9XJ8Qk9Zn8ZXa7x8Y59TG9Nyakia78aKo8B7av77CR8cJ6D56fB8Ct6iS6kV7ZG6zM6MY6BR7cz6CR6UI7yW7Cu9sWaJx'}


def sb(n, t):
    return ("sbuf", [128, n], t)


SCRATCH = {"vt": sb(W, BF), "ki": sb(W, I32), "kt": sb(2 * TW, F), "ni": sb(R, I32), "ys": sb(RO * 2 * R, BF),
           "e32": sb(512, BF), "pb": sb(4, I32), "p4": sb(4, I32),
           "yr": sb(RO * R * 16, BF), "pf": sb(RO * R, H), "po": sb(RO * R, H), "pu": sb(R, U16),
           "pl": sb(R, F), "ph": sb(R, F), "fa": sb(256, F), "fc": sb(256, F), "fh": sb(W, H), "col": sb(144, F),
           "pj": sb(16, I32), "pa": sb(16, I32), "ka": sb(16, F), "cc": sb(16, F), "cs": sb(32, F),
           "idf": sb(128, F), "be": sb(8, BF), "bf": sb(8, BF), "bg": sb(8, BF), "zs": sb(144, BF),
           "sm": sb(1024, BF), "end": sb(8, U16), "dd": sb(2048, BF), "wg": sb(16, F), "wh": sb(16, F)}
for _n in ("colk", "colg", "idb", "nid", "nst", "blk", "gt", "gb", "lz", "rot", "nri", "bigm", "one", "ez", "bb", "nbb",
           "neg", "big", "bid"):
    SCRATCH[_n] = sb(128, BF)
PER = {"vg": (16, BF), "ab": (16, BF), "kg": (16, H), "js": (16, H), "cm": (16, BF), "ks": (1, BF), "xo": (1, H),
       "eq": (1, BF), "ne": (1, BF), "sg": (1, BF), "r": (1, H), "kf": (1, H), "tp": (1, H), "mx": (1, H), "jp": (1, F),
       "ea": (2, BF), "nf": (2, BF), "ko": (1, H)}
SLOT = {"pm": (128, F), "pn": (128, F), "st": (144, BF), "oo": (8, U16), "o3": (8, H), "ot": (8, U16), "of": (16, U16)}
for _n in PER:
    SCRATCH[_n] = sb(R * PER[_n][0], PER[_n][1])
for _n in SLOT:
    SCRATCH[_n] = sb(2 * SLOT[_n][0], SLOT[_n][1])
for _b in range(8):
    SCRATCH["ps%d" % _b] = ("psum", [128, 512], F)
TILE = {"key": (0, 0), "oot": (0, 0), "dup": (0, 8), "ksp": (0, 128), "x": (0, 256), "pps": (1, 256),
        "cnt": (1, 0), "jpp": (1, 0), "zz": (1, 128), "otp": (1, 128), "p1p": (1, 256), "orep": (1, 384), "bak": (1, 384)}
NWIDE = 4

SEMAPHORES = (["sD", "sA", "sP", "sG", "sent", "stk", "st0", "st1"] + ["ld%d" % i for i in range(5)]
              + ["ck%d" % t for t in range(RO)] + ["ay%d" % t for t in range(RO)]
              + ["ap%d%d" % (t, c) for t in range(RO) for c in range(2)])


def A(name, c0=0, c1=None, step=1, p0=0, p1=128):
    if c1 is None:
        c1 = SCRATCH[name][1][1]
    return ("ap", name, p0, p1, c0, c1, step)


def IND(win, off):
    return ("ind", win, off)


def ncol(a):
    if a[0] == "ind":
        return 16 * ncol(a[2])
    return len(range(a[4], a[5], a[6]))


def isap(a):
    return isinstance(a, tuple) and len(a) > 0 and a[0] in ("ap", "ind")


def config(st):
    over = {}
    for t in range(RO):
        for c in range(2):
            over[(t, c)] = dict({"yr": "G", "bl": 1, "pn": "S", "bs": 0, "pp": 1},
                                **dict(st["per"][c], **(st["r0"][c] if t == 0 else st["r3"][c] if t == RO - 1 else {})))
    return dict(over=over, **st.get("x", {}))


def program(cfg):
    ops = []
    n, m = CH, CH // 16
    at = [-1, 0]

    def op(q, ins, name):
        ops.append({"q": q, "ins": ins if isinstance(ins, list) else [ins], "name": name, "at": tuple(at)})

    def pick(kind):
        return cfg["over"][(at[0], at[1])][kind]

    def used(kind, q):
        return any(q in v[kind] for v in cfg["over"].values())

    def pieces(kind):
        s = pick(kind)
        out = []
        for i, q in enumerate(s):
            a, b = n * i // len(s), n * (i + 1) // len(s)
            if q == "+":
                out[-1] = (out[-1][0], out[-1][1], b)
            else:
                out.append((q, a, b))
        return out

    def nm(o): return o[1] if o[0] == "ap" else "scat"
    def tt(o, a, b, f): op("D", ("tt", o, a, b, f), nm(o))
    def ts(o, a, s1, s2, f0, f1=None): op("D", ("ts", o, a, s1, s2, f0, f1), nm(o))
    def act(o, a, f, b=0.0, s=1.0): op("A", ("act", o, a, f, b, s), nm(o))
    def cp(o, a, q="D"):
        if q == "D":
            op("D", ("cp", o, a), nm(o))
        elif q == "G":
            op("G", ("rep", o, a), nm(o))
        else:
            act(o, a, "Copy")
    def ms(o, v): op("D", ("ms", o, v), nm(o))
    def mm(terms, name, first=True, last=True):
        op("P", [("mm", o, l, r, first and i == 0, last and i == len(terms) - 1) for i, (o, l, r) in enumerate(terms)], name)
    def iota(o, pat, b, cm): op("G", ("iota", o, pat, b, cm), nm(o))
    def row(name, k=128): return A(name, 0, k, 1, 0, 1)
    def cs(i): return A("cs", i, i + 1)

    op("S", ("dma", A("ni"), A("nam", 0, R), "ld1"), "ldn")
    op("A", ("dma", A("ys", 0, R), A("seen", 0, R), "ld2"), "lds")
    op("A", ("dma", A("vt"), A("val", 0, W), "ld0"), "ldv")
    op("S", ("dma", A("ki", 0, W // 2), A("clk", 0, W // 2), "ld3"), "ldk")
    op("S", ("dma", A("ki", W // 2, W), A("clk", W // 2, W), "ld4"), "ldk")
    iota(A("pj"), [[1, 16]], 0, 1)
    iota(A("col"), [[1, 144]], 0, 0)
    iota(A("colk"), [[0, 8], [1, 16]], 0, 0)
    iota(A("colg"), [[16, 8], [0, 16]], 0, 0)
    ts(A("pa"), A("pj"), 15, None, "bitwise_and")
    cp(A("ka"), A("pa"))
    acol = A("ka", 0, 1)
    tt(cs(0), A("pj", 0, 1), A("pa", 0, 1), "subtract")
    g16 = cs(0)
    ts(A("cc"), A("ka"), g16, None, "add")
    ts(cs(2), g16, 15.0, None, "add")
    if used("sg", "A"):
        ts(cs(3), acol, -1024.0, 1025.0 - W, "mult", "add")
    if used("sg", "D"):
        ts(cs(4), acol, 0.0, 1.0 - W, "mult", "add")
    ts(cs(6), acol, float(W), None, "add")
    c128, me = A("col", 0, 128), A("cc", 0, 1)
    ts(A("idb"), c128, me, None, "is_equal")
    act(A("nid"), A("idb"), "Copy", 0.0, -1.0)
    ts(A("be"), A("colg", 0, 128, 16), g16, 16.0, "is_equal", "mult")
    if used("re", "D"):
        act(A("bf"), A("be"), "Copy", 0.0, 2.0)
        act(A("bg"), A("be"), "Copy", 0.0, -1.0)
    ms(row("one"), 1.0)
    ms(row("neg"), -1.0)
    ms(row("big"), 4096.0)
    ms(A("bigm"), 0.0)
    ms(A("bigm", 0, 128, 16), 1048576.0)
    ts(A("end"), A("col", 0, 8), 16.0, 15.0, "mult", "add")
    act(row("ez"), row("colk"), "Relu", 1.0, -1.0)
    ts(A("blk"), A("colg"), g16, None, "is_equal")
    act(A("bb"), A("blk"), "Copy", 0.0, 4096.0)
    act(A("nbb"), A("blk"), "Copy", 0.0, -4096.0)
    act(A("idf"), A("idb"), "Copy")
    act(A("nst"), A("idb"), "Copy", 0.0, -16.0)
    ts(A("gt"), A("colk"), acol, None, "is_gt")
    tt(A("gb"), A("gt"), A("blk"), "mult")
    tt(A("gt"), A("idb"), A("gb"), "subtract")
    act(A("lz"), A("gt"), "Copy", 0.0, 1024.0)
    ts(A("rot"), c128, A("cc", 1, 2), None, "is_equal")
    ts(A("nri"), c128, A("cc", 15, 16), -1.0, "is_equal", "mult")
    ts(A("zs"), A("col"), cs(2), None, "is_equal")
    ms(A("sm"), 2048.0)
    ms(A("sm", 0, 1024, 16), 0.0)
    ts(A("wg"), A("col", 0, 16), acol, 4096.0, "is_lt", "mult")
    ts(A("wh"), A("col", 0, 16), acol, 4096.0, "is_equal", "mult")
    tt(A("wg"), A("wg"), A("wh"), "subtract")
    for a in range(16):
        o = A("dd", 128 * a, 128 * a + 128)
        if cfg.get("dd", "DDDA")[a % 4] == "D":
            ts(o, A("idb"), A("wg", a, a + 1), None, "mult")
        else:
            act(o, A("idb"), "Copy", 0.0, A("wg", a, a + 1))
    if any(v["bl"] == 2 for v in cfg["over"].values()):
        act(A("bid"), A("idb"), "Copy", 0.0, 4096.0)
        op("D", ("ts", cs(7), acol, W + 16.0, None, "add", None), "c7")
    ts(A("p4", 0, 1), A("pj", 0, 1), 3, None, "bitwise_and")
    for kv in sorted(set(4 * v["cm"].count("D") for v in cfg["over"].values())):
        i = 8 + kv // 2
        ts(cs(i), A("p4", 0, 1), float(kv // 4), 4.5, "is_lt", "mult")
        ts(cs(i), cs(i), 7.0, None, "add")
        if used("sg", "A"):
            ts(cs(i + 1), cs(i), -1.0, None, "mult")
    for c in range(2):
        ms(A("st", 144 * c, 144 * c + 16), 1.0)
    if used("pn", "D") or used("pn", "A"):
        ms(A("pn"), 0.0)
    for k0 in (0, TW):
        ms(A("kt", k0, k0 + PAD), 0.0)
        ms(A("kt", k0 + PAD + W, k0 + TW), 0.0)
    ts(A("pb", 0, 1), A("pj", 0, 1), 31, None, "bitwise_and")
    ts(cs(1), A("pb", 0, 1), 16.0, None, "mult")
    for j in range(4):
        ts(A("e32", 128 * j, 128 * j + 128), A("colg"), 128.0 * j, cs(1), "add", "is_equal")
    mm([(A("ps0", 128 * h, 128 * h + 128), A("ys", 128 * h, 128 * h + 128), A("idb")) for h in (1, 0)], "yT")
    cp(A("ys", R, 2 * R), A("ps0", 0, R), "A")
    op("G", ("rdma", A("ys", 2 * R, 3 * R), A("ys", 0, R), HOP, "ay1"), "sendy")
    op("G", ("rdma", A("ys", 3 * R, 4 * R), A("ys", R, 2 * R), HOP, "ay0"), "sendy")
    for t in range(2, RO):
        op("G", ("rdma", A("ys", 2 * R * t, 2 * R * t + 2 * R), A("ys", 0, 2 * R), HOP * t, "ay%d" % t), "sendy")
    for h in range(2):
        cp(A("kt", PAD + 1024 * h, PAD + 1024 * h + 1024), A("ki", 1024 * h, 1024 * h + 1024), cfg.get("kc", "DD")[h])

    def sel(a): return A("zs", 15 - a, 143 - a)
    wide = [0]

    def turn():
        wide[0] += 1
        return "ps%d" % (wide[0] % NWIDE)

    for t in range(RO):
        at[:] = [t, 0]
        k0, k1 = TW * (t % 2), TW * (1 - t % 2)
        KT = A("kt", k0 + PAD, k0 + PAD + W)
        op("S", ("dma", A("kt", k1 + PAD, k1 + PAD + W), KT, "ck%d" % t), "cpk")
        runs = []
        for c in (1, 0):
            at[:] = [t, c]
            for q, a, b in pieces("vg")[::-1]:
                if q != "D":
                    continue
                lo, hi = n * c + a, n * c + b
                if runs and runs[-1][0] == pick("yr") and runs[-1][1] == hi and (pick("yr") == "G" or b < n):
                    runs[-1] = (pick("yr"), lo, runs[-1][2])
                else:
                    runs.append((pick("yr"), lo, hi))
        for q, lo, hi in runs:
            at[:] = [t, int(hi > n)]
            for k in range(16):
                cp(A("yr", 16 * (t * R + lo) + k, 16 * (t * R + hi), 16), A("ys", 2 * R * t + lo, 2 * R * t + hi), q)
        for c in (1, 0):
            at[:] = [t, c]
            def B(name, a=0, b=None, step=1):
                w = PER[name][0] * n if name in PER else SLOT[name][0]
                return A(name, w * c + a, w * c + (w if b is None else b), step)
            def S(name, a=0, b=n, step=1):
                return A("ps%d" % (NWIDE + 2 * c + TILE[name][0]), TILE[name][1] + a, TILE[name][1] + b, step)
            key, ksp, orep, pps, cnt, zz, p1p, bak, jpp, x = (
                S(k) for k in ("key", "ksp", "orep", "pps", "cnt", "zz", "p1p", "bak", "jpp", "x"))
            oot, otp, dup = S("oot", 0, m), S("otp", 0, m), S("dup", 0, m)
            pc = t * R + n * c
            PF = A("pf", pc, pc + n)
            def PU(a, b): return A("pu", n * c + a, n * c + b)
            if t == 0:
                cp(PU(0, n), A("ni", pc, pc + n))
                cp(PF, A("ni", pc, pc + n))
            else:
                cp(PU(0, n), PF)
            if pick("pp"):
                mm([(pps, A("idb"), PF)], "pps")
            head = [(key, row("one"), row("colk"))]
            both = "D" in pick("re")
            runs = []
            for (q, a, b), r in zip(pieces("vg"), pick("re")):
                vg = B("vg", 16 * a, 16 * b)
                if q == "D":
                    tt(vg, IND(A("vt"), PU(a, b)), A("yr", 16 * (pc + a), 16 * (pc + b)), "subtract")
                    if r == "+" and runs[-1][3] is None:
                        runs[-1][2] = b
                        continue
                    src = None
                else:
                    cp(vg, IND(A("vt"), PU(a, b)), q.upper())
                    src = A(turn())
                    y0 = 2 * R * t + R + n * c
                    mm([(src, A("ys", y0, y0 + 128, 1, a, a + 32), A("e32", 0, 512, 1, a, a + 32)), (src, A("nid"), vg)], "dv")
                runs.append([runs[-1][0] if r == "+" else r, a, b, src])
            for r, a, b, src in runs:
                ab = B("ab", 16 * a, 16 * b)
                src, sign = (src, -1.0) if src else (B("vg", 16 * a, 16 * b), 1.0)
                if r == "A":
                    act(ab, src, "Relu" if both else "Abs", 0.0, sign)
                else:
                    ts(ab, src, sign, 0.0, "mult", "max")
            if both:
                mm(head + [(S("key", k, 128, 16), B("vg", k, 16 * n, 16), A("bg")) for k in range(16)], "key", True, False)
            mm(([] if both else head)
               + [(S("key", k, 128, 16), B("ab", k, 16 * n, 16), A("bf" if both else "be")) for k in range(16)],
               "key", not both, True)
            op("D", [("scan", B(u), A("bigm"), key, 0.0, "add", "min") for u in ("pm", "pn")[:1 + (pick("pn") == "S")]], "pm")
            if pick("pn") != "S":
                cp(B("pn", 15, 128, 16), B("pm", 15, 128, 16), pick("pn"))
            tt(B("st", 16, 144), IND(B("pn"), A("end")), B("pm"), "is_equal")
            mm([(ksp, row("ez"), row("one")), (ksp, B("st", 16, 144), A("idb")), (ksp, B("st", 15, 143), A("nid"))], "ksp")
            tt(B("xo"), ksp, PF, "mult")
            mm([(oot, sel(a), B("xo", a, n, 16)) for a in range(16)], "oot")
            cp(B("oo"), oot)
            cp(B("ko"), IND(KT, B("oo")), pick("ko"))
            cp(B("ks"), ksp, pick("ks"))
            cp(B("o3"), oot, pick("o3"))
            if pick("eq") == "D":
                mm([(orep, A("blk"), B("xo"))], "orep")
                tt(B("eq"), orep, PF, "is_equal")
            else:
                mm([(orep, A("nid"), PF), (orep, A("blk"), B("xo"))], "orep")
                act(B("ne"), orep, "Abs")
                act(B("eq"), B("ne"), "Relu", 1.0, -1.0)
            kv = 4 * pick("cm").count("D")
            if kv:
                kop = turn()
                mm([(A(kop, j, 4 * n, 4), A("idb"), B("ko")) for j in range(4)], "kop")
            pairs = [(S("x", n + 16 * j, n + 16 * j + 16), 32 * j) for j in range(m // 2 if pick("bl") == 2 else 0)]
            mm([(x, A("blk"), B("xo"))] + [(o, A("blk"), B("xo", a, a + 16)) for o, a in pairs]
               + [(S("x", a, n, 16), A("nid"), B("o3")) for a in range(16)]
               + [(S("x", n + a, n + 64, 16), A("nid"), B("o3", 1, m, 2)) for a in range(16 if pairs else 0)], "x", True, False)
            for q, a, b in pieces("kg"):
                cp(B("kg", 16 * a, 16 * b), IND(KT, PU(a, b)), q)
            for j in range(pick("sj")):
                a, b = 16 * n * j // pick("sj"), 16 * n * (j + 1) // pick("sj")
                op("D", ("scan", B("js", a, b), A("sm", 0, b - a), B("kg", a, b), 0.0, "min", "max"), "js")
            tt(B("mx"), pps if pick("pp") else PF, B("js", 15, 16 * n, 16), "max")
            runs = [int(k) for k in {0: "0123", 4: "1023", 8: "0213", 12: "0312", 16: "0123"}[kv]]
            for u in runs:
                a, b = 4 * u, 4 * u + 4
                if a < kv:
                    tt(B("cm", n * a, n * b), B("kg", u, 16 * n, 4), A(kop), "is_ge")
                else:
                    wb = turn()
                    mm([(A(wb), A("idb"), B("kg", u, 16 * n, 4))], "dk", True, False)
                    mm([(A(wb, j, 4 * n, 4), A("nid"), B("ko")) for j in range(4)], "do", False, True)
                    act(B("cm", n * a, n * b), A(wb), "Sign", 0.5, 1.0)
                terms = [(cnt, sel(u + 4 * j), B("cm", n * a + j, n * b, 4)) for j in range(4)]
                mm(([(cnt, A("nst"), B("eq"))] if u == runs[2] else []) + terms, "cnt", u == runs[0], u == runs[3])
            if pick("sg") == "A":
                act(B("sg"), cnt, "Sign", cs(9 + kv // 2), 1.0)
            else:
                ts(B("sg"), cnt, cs(8 + kv // 2), 2.0, "is_ge", "mult")
            mm([(zz, A("idb"), PF), (zz, A("lz"), B("sg"))], "zz")
            hb = cs(3 if pick("sg") == "A" else 4)
            if pick("r") == "A":
                act(B("r"), zz, "Relu", hb, 1.0)
            else:
                ts(B("r"), zz, hb, 0.0, "add", "max")
            mm([(otp, sel(a), B("r", a, n, 16)) for a in range(16)], "otp")
            ts(B("ot"), otp, PAD - 1.0, None, "add")
            mm([(p1p, row("neg"), row("one")), (p1p, A("nri"), PF), (p1p, A("blk"), B("r"))], "p1p")
            tt(B("tp"), p1p, B("ks"), "mult")
            if pick("jp") == "A":
                mm([(jpp, A("idb"), B("mx")), (jpp, A("nbb"), B("r"))], "jpp")
                act(B("jp"), jpp, "Relu")
            else:
                mm([(jpp, row("big"), row("one")), (jpp, A("nbb"), B("r"))], "jpp")
                tt(B("jp"), jpp, B("mx"), "min")
            tt(B("kf"), IND(A("kt", k0, k0 + PAD + W), B("ot")), B("ks"), "mult")
            terms = [(bak, A("idb"), PF), (bak, A("nid"), B("xo")), (bak, A("rot"), B("tp")), (bak, A("idb"), B("kf"))]
            if pick("bs"):
                mm(terms[:3], "bah", True, False)
            mm(terms[3 * pick("bs"):], "bak", not pick("bs"), True)
            if t < RO - 1:
                src, dst, hop = A("po", pc, pc + n), A("pf", pc + R, pc + R + n), HOP
            else:
                src, dst, hop = A("pl", n * c, n * c + n), A("ph", n * c, n * c + n), -HOP * t
            tt(src, bak, B("jp"), "max")
            op("G", ("rdma", dst, src, hop, "ap%d%d" % (t, c)), "sendp")
            if t == RO - 1:
                op("S", ("dma", A("yp", n * c, n * c + n), dst, "st%d" % c), "stp")
            mm([(x, A("bb"), B("r"))] + [(o, A("bb"), B("r", a, a + 16)) for o, a in pairs], "x", False, True)
            xw = n + 16 * len(pairs)
            if pick("ea") == "D":
                ts(B("ea", 0, xw), S("x", 0, xw), 0.0, None, "is_equal")
            else:
                act(B("nf", 0, xw), S("x", 0, xw), "Abs")
                act(B("ea", 0, xw), B("nf", 0, xw), "Relu", 1.0, -1.0)
            mm([(dup, row("big"), row("one", m)), (dup, A("idb"), B("o3"))]
               + [(dup, A("dd", 128 * a, 128 * a + 128), B("ea", a, n, 16)) for a in range(16)]
               + [(S("dup", 1, m, 2), A("bid"), B("ea", n + a, xw, 16)) for a in range(16 if pairs else 0)], "dup")
            if pairs:
                op("D", [("ts", B("of", j, m, 2), S("dup", j, m, 2), cs(6 + j), None, "min", None) for j in range(2)], "of")
            else:
                ts(B("of", 0, 2 * m, 2), dup, cs(6), None, "min")
            u = pick("bl")
            for b in range(m // u - 1, -1, -1):
                cp(IND(A("kt", k1 + PAD, k1 + TW), B("of", 2 * b, 2 * b + u)), B("js", 256 * u * b + 15, 256 * u * (b + 1), 16))
    at[:] = [RO, 0]
    def kcol(b, e): return A("kt", PAD + 256 * b, PAD + 256 * e)
    fo = A("ps0", 0, 256)
    mm([(fo, A("idf"), kcol(0, 1))], "fold", True, False)
    runs = [("A", 1, 3), ("D", 4, 6), ("A", 3, 4), ("D", 6, 8)]
    for q, a, b in runs:
        cp(A("fh", 256 * a, 256 * b), kcol(a, b), q)
        mm([(fo, A("idb"), A("fh", 256 * j, 256 * j + 256)) for j in range(a, b)], "fold", False, b == 8)
    cp(A("fc"), fo, "A")
    op("S", ("dma", A("yk", 0, 256), A("fc"), "stk"), "stk")
    return ops


def links(ops):
    hist, lastp = {}, {}
    for x, o in enumerate(ops):
        wr, rd = set(), set()
        for i in o["ins"]:
            for n, a in enumerate(y for y in i[1:] if isap(y)):
                if a[0] == "ind":
                    rd.add((a[2][1], a[2][4], a[2][5]))
                    a = a[1]
                (rd if n else wr).add((a[1], a[4], a[5]))
        o["banks"] = sorted(set(r[0] for r in wr | rd if r[0].startswith("ps")))
        o["dma"] = o["ins"][0][0] in ("dma", "rdma")
        dep = set()
        for regs, mine in ((rd, False), (wr, True)):
            for nm, lo, hi in regs:
                for y, l2, h2, w2 in hist.get(nm, []):
                    if l2 < hi and lo < h2 and (mine or w2) and not (nm == "yr" and mine):
                        dep.add(y)
        if o["q"] == "P":
            for b in o["banks"]:
                if b in lastp:
                    dep.add(lastp[b])
                lastp[b] = x
        o["dep"] = sorted(dep)
        for regs, mine in ((rd, False), (wr, True)):
            for nm, lo, hi in sorted(regs):
                h = hist.setdefault(nm, [])
                if mine and nm != "yr":
                    h[:] = [e for e in h if not (lo <= e[1] and e[2] <= hi)]
                h.append((x, lo, hi, mine))


def waits(ops, o, last):
    q = o["q"]
    wait = [y for y in o["dep"] if ops[y]["q"] != q or q != "P"]
    for b in o["banks"]:
        wait += [y for q2, y in last.get(b, {}).items() if q2 != q]
    return wait


AL = "0123456789abcdefghijklmnopqrstuvwxyzABCDEFGHIJKLMNOPQRSTUVWXYZ"


def order_of(ops, st):
    keys, cnt = [], {}
    for o in ops:
        t, c = o["at"]
        i = cnt.get((o["name"], t, c), 0)
        cnt[(o["name"], t, c)] = i + 1
        keys.append(("0" if t <= 0 else "e" if t >= RO else "") + o["name"] + "0123456789ABCDEFGHIJKLMNOPQRSTUVWXYZ"[i]
                    + ("ba"[c] if 0 <= t < RO else ""))
    z = st["phi"]
    phi = {k: (AL.index(z[3 * i]) * 3844 + AL.index(z[3 * i + 1]) * 62 + AL.index(z[3 * i + 2])) * 2.0
           for i, k in enumerate(sorted(set(keys)))}
    rank = [phi[k] + (o["at"][0] - 2) * st["T"] * (0 < o["at"][0] < RO) for k, o in zip(keys, ops)]
    seq, done = [], set()
    todo = sorted(range(len(ops)), key=lambda x: (rank[x], x))
    while todo:
        x = next(x for x in todo if all(y in done for y in ops[x]["dep"]))
        todo.remove(x)
        done.add(x)
        seq.append(x)
    return seq


def plan(st):
    ops = program(config(st))
    links(ops)
    order = {q: [] for q in "DAPGS"}
    total = {q: 0 for q in "DAPG"}
    seen = {q: {} for q in order}
    last = {}
    for i, x in enumerate(order_of(ops, st)):
        o = ops[x]
        q = o["q"]
        o["pos"] = i
        wait = waits(ops, o, last)
        for b in o["banks"]:
            last.setdefault(b, {})[q] = x
        o["need"] = []
        for y in sorted(set(wait), key=lambda y: -ops[y]["pos"]):
            sem, v = ops[y]["sig"]
            if v > seen[q].get(sem, 0):
                o["need"].append((sem, v))
                for s, u in ops[y]["knows"].items():
                    seen[q][s] = max(u, seen[q].get(s, 0))
        if not o["dma"]:
            total[q] += 1
            o["sig"] = ("s" + q, total[q])
        else:
            o["sig"] = (o["ins"][0][3], 16) if o["ins"][0][0] == "dma" else (o["ins"][0][4], 1)
        o["knows"] = dict({} if o["ins"][0][0] == "rdma" else seen[q], **{o["sig"][0]: o["sig"][1]})
        order[q].append(x)
    return ops, order, total


MEMO = {}


def rank_program(g, core, T, topo):
    rank = T.rank_of(core)
    if rank is None:
        return
    if "plan" not in MEMO:
        MEMO["plan"] = plan(ST)
    ops, order, total = MEMO["plan"]
    cores = T.cores
    queue = {"D": g.vector, "A": g.scalar, "P": g.tensor, "G": g, "S": g.sync}
    alu = {"add": AluOpType.add, "subtract": AluOpType.subtract, "mult": AluOpType.mult, "max": AluOpType.max,
           "min": AluOpType.min, "is_equal": AluOpType.is_equal, "is_lt": AluOpType.is_lt, "is_gt": AluOpType.is_gt,
           "is_ge": AluOpType.is_ge, "bitwise_and": AluOpType.bitwise_and}
    fn = {"Copy": ActivationFunctionType.Copy, "Abs": ActivationFunctionType.Abs, "Sign": ActivationFunctionType.Sign,
          "Relu": ActivationFunctionType.Relu}

    def ap(a):
        if not isap(a):
            return a
        if a[0] == "ind":
            return ap(a[1]).indirect(ap(a[2]))
        if a[6] == 1:
            return T[a[1]][a[2]:a[3], a[4]:a[5]]
        return T[a[1]][a[2]:a[3], a[4]:a[5]:a[6]]

    arrive = {o["ins"][0][4]: len(topo.engines(cores[(rank - o["ins"][0][3]) % NR], core))
              for o in ops if o["ins"][0][0] == "rdma"}
    sent = 0
    for q in "SAGPD":
        e = queue[q]
        for x in order[q]:
            o = ops[x]
            for sem, v in o["need"]:
                e.wait_ge(T.sem[sem], arrive.get(sem, v))
            for i in o["ins"]:
                k = i[0]
                a = [ap(y) for y in i[1:]]
                if k == "dma":
                    e.dma_start(a[0], a[1]).then_inc(T.sem[i[3]], 16)
                    continue
                if k == "rdma":
                    dst = cores[(rank + i[3]) % NR]
                    rid, pid = topo.addr(dst, core)
                    e.remote_dma(a[0], a[1], T.sem[i[4]], T.sem.sent, pid, rid, topo.mask(core, dst))
                    sent += len(topo.engines(core, dst))
                    continue
                if k == "mm":
                    h = e.matmul(a[0], a[1], a[2], a[3], a[4])
                elif k == "tt":
                    h = e.tensor_tensor(a[0], a[1], a[2], alu[a[3]])
                elif k == "ts":
                    if a[5] is None:
                        h = e.tensor_scalar(a[0], a[1], a[2], None, alu[a[4]])
                    else:
                        h = e.tensor_scalar(a[0], a[1], a[2], a[3], alu[a[4]], alu[a[5]])
                elif k == "cp":
                    h = e.tensor_copy(a[0], a[1])
                elif k == "scan":
                    h = e.tensor_tensor_scan(a[0], a[1], a[2], a[3], alu[a[4]], alu[a[5]])
                elif k == "rep":
                    h = e.affine_select(a[0], a[1], [[0, ncol(i[1])]], AluOpType.is_gt, 0.0, 1, 0)
                elif k == "ms":
                    h = e.memset(a[0], a[1])
                elif k == "act":
                    h = e.activation(a[0], a[1], fn[a[2]], bias=a[3], scale=a[4])
                elif SCRATCH[i[1][1]][2] == I32:
                    h = e.iota(a[0], a[1], a[2], a[3])
                else:
                    h = e.iota(a[0], a[1], a[2], a[3], allow_small_or_imprecise_dtypes=True)
                if i is o["ins"][-1]:
                    h.then_inc(T.sem["s" + q], 1)
    for q in "DAPG":
        g.wait_ge(T.sem["s" + q], total[q])
    g.wait_ge(T.sem.sent, sent)
    for s in ("stk", "st0", "st1"):
        g.wait_ge(T.sem[s], 16)
